import numpy as np
import ml_dtypes


def mxq(x, axis, fmt="e4m3"):
    dtype, down = {"e4m3": (ml_dtypes.float8_e4m3fn, 7), "e5m2": (ml_dtypes.float8_e5m2, 14)}[fmt]
    v = np.moveaxis(np.asarray(x, np.float32).astype(ml_dtypes.bfloat16).astype(np.float64), axis, -1)
    blocks = v.reshape(v.shape[:-1] + (-1, 32))
    amax = np.abs(blocks).max(-1, keepdims=True)
    byte = np.maximum(np.where(amax > 0, np.frexp(amax)[1] - 1 + 127, 0) - down, 1)
    scale = np.exp2(byte - 127.0)
    codes = (blocks / scale).astype(np.float32).astype(dtype).astype(np.float64)
    return np.moveaxis((codes * scale).reshape(v.shape), -1, axis)


WIDE = False


def mx_kscale(k):
    if not WIDE:
        return np.ones(k)
    levels = np.array([10, -10, 5, -5, 0])
    if k % 512:
        return np.exp2(np.random.permutation(np.resize(levels, k // 32))).repeat(32)
    a = np.empty((k // 512, 16))
    for p in range(k // 512):
        a[p, :8] = np.random.permutation(np.resize(levels, 8))
        for g in range(8):
            far = levels[np.abs(levels - a[p, g]) >= 10]
            a[p, g + 8] = far[np.random.randint(len(far))]
    return np.exp2(a.ravel()).repeat(32)


def f64(x):
    return np.asarray(x).astype(np.float64)


def striped(idx):
    return np.tile(np.asarray(idx).reshape(-1, 16).T, (8, 1)).astype(np.uint16)


def unstriped(offs):
    return offs[:16].T.reshape(-1).astype(np.int64)


E2M1 = np.array([0.0, 0.5, 1.0, 1.5, 2.0, 3.0, 4.0, 6.0, -0.0, -0.5, -1.0, -1.5, -2.0, -3.0, -4.0, -6.0])


def pack_weight(w, fmt):
    k, n = w.shape
    w = f64(np.asarray(w, np.float32).astype(ml_dtypes.bfloat16)).reshape(k // 32, 32, n)
    amax = np.abs(w).max(1)
    if fmt == "e4m3":
        byte = np.frexp(amax)[1] - 1 + 127 - 7
    else:
        mant, ex = np.frexp(amax / 6.0)
        byte = np.where(mant > 0.5, ex, ex - 1) + 127
    byte = np.clip(np.where(amax > 0, byte, 1), 1, 254)
    scaled = (w * np.exp2(127.0 - byte)[:, None, :]).reshape(k, n).astype(np.float32)
    by_word = np.ascontiguousarray(scaled.reshape(k // 512, 128, 4, n).transpose(0, 1, 3, 2))
    if fmt == "e4m3":
        words = by_word.astype(ml_dtypes.float8_e4m3fn).view(np.uint8)
    else:
        c = by_word.astype(ml_dtypes.float4_e2m1fn).view(np.uint8) & 0xF
        words = (c[..., 0::2] | (c[..., 1::2] << 4)).reshape(k // 512, 128, 2 * n)
    return np.ascontiguousarray(words), np.ascontiguousarray(byte.astype(np.uint8).reshape(k // 512, 16, n))


def unpack_weight(words, scales, fmt):
    g, _, n = scales.shape
    words = np.ascontiguousarray(words).reshape(g, 128, n, -1)
    if fmt == "e4m3":
        vals = words.view(ml_dtypes.float8_e4m3fn).astype(np.float64)
    else:
        nib = np.empty((g, 128, n, 4), np.uint8)
        nib[..., 0::2] = words & 0xF
        nib[..., 1::2] = words >> 4
        vals = E2M1[nib]
    vals = vals * np.repeat(np.exp2(scales.astype(np.float64) - 127.0), 8, axis=1)[..., None]
    return vals.transpose(0, 1, 3, 2).reshape(g * 512, n)


B, N, T, D, NQ = 1, 512, 2048, 512, 512
DV = 512


def sgn(shape):
    return np.random.uniform(0.5, 2.0, shape) * np.where(np.random.standard_normal(shape) < 0, -1.0, 1.0)


def setup_inputs():
    n = np.random.standard_normal
    idx = np.random.permutation(T)[:B * N]
    s = mx_kscale(D)[:, None]
    u = mx_kscale(N)
    ut = np.ones(T)
    ut[idx] = u
    kp = pack_weight(n((D, T)) / s, "e4m3")
    cp = pack_weight(n((D, T)) / s, "e4m3")
    return {
        "qT": (n((B, D, NQ)) * s * (1.00 / np.sqrt(D))).astype(np.float32),
        "k_words": kp[0],
        "k_scales": kp[1],
        "c_words": cp[0],
        "c_scales": cp[1],
        "vT": (n((DV, T)) / ut).astype(np.float32),
        "ls": (np.random.uniform(7.0, 7.6, (B, 1, NQ))).astype(np.float32),
        "lm": (np.random.uniform(0.2, 0.8, (B, 1, NQ))).astype(np.float32),
        "l2": (np.random.uniform(7.0, 7.6, (B, 1, NQ))).astype(np.float32),
        "us": (sgn((B, N, 1)) * u[:, None]).astype(np.float32),
        "offs": striped(idx),
    }


def reference(qT, k_words, k_scales, c_words, c_scales, vT, ls, lm, l2, us, offs):
    idx = unstriped(offs)
    pick = lambda x, which: x[:, which].reshape(x.shape[0], B, -1).transpose(1, 0, 2)
    k = unpack_weight(k_words, k_scales, "e4m3")
    kg = pick(k, idx)
    c = unpack_weight(c_words, c_scales, "e4m3")
    cg = pick(c, idx)
    qq = mxq(f64(qT), 1, "e4m3")
    a = kg.transpose(0, 2, 1) @ qq
    z = cg.transpose(0, 2, 1) @ qq
    y = (np.exp(a - f64(ls)) - f64(lm) * np.exp(z - f64(l2))) * f64(us)
    wq = mxq(y, 1, "e4m3")
    o = wq.transpose(0, 2, 1) @ mxq(pick(f64(vT), idx).transpose(0, 2, 1), 1, "e4m3")
    ms = np.mean(np.square(o), axis=-1, keepdims=True)
    r_ = o / np.sqrt(ms + 1e-05)
    return r_

@@ -1,0 +1,224 @@
+from contextlib import ExitStack
+
+import concourse.mybir as mybir
+from concourse.masks import make_identity
+
+F32 = mybir.dt.float32
+BF16 = mybir.dt.bfloat16
+I32 = mybir.dt.int32
+U32 = mybir.dt.uint32
+U16 = mybir.dt.uint16
+U8 = mybir.dt.uint8
+FP8X4 = mybir.dt.float8_e4m3fn_x4
+ACT = mybir.ActivationFunctionType
+ALU = mybir.AluOpType
+
+P = 128
+PACK = 4
+T = 2048
+N = 512
+NQ = 512
+DV = 512
+EPS = 1e-05
+FLOPS = 3 * 2 * 512 * 512 * 512
+
+
+def tile_attend_at_diff_topk_kernel(tc, qT, k_words, k_scales, c_words, c_scales, vT, ls, lm, l2, us, offs, out):
+    nc = tc.nc
+    with ExitStack() as ctx:
+        keep = ctx.enter_context(tc.tile_pool(name="keep", bufs=1))
+        big = ctx.enter_context(tc.tile_pool(name="big", bufs=3))
+        ring = ctx.enter_context(tc.tile_pool(name="ring", bufs=2))
+        work = ctx.enter_context(tc.psum_pool(name="work", bufs=4))
+        acc = ctx.enter_context(tc.psum_pool(name="acc", bufs=1))
+
+        offsets = keep.tile([P, N // 16], U16, name="offsets")
+        nc.sync.dma_start(offsets[:], offs)
+
+        q_raw = big.tile([P, PACK, NQ], F32, tag="big", name="q_raw")
+        nc.sync.dma_start(out=q_raw[:], in_=qT[0].rearrange("(p j) q -> p j q", j=PACK))
+
+        def load_words(words, name):
+            pool_words = big.tile([P, T], I32, tag="big", name=name)
+            nc.sync.dma_start(out=pool_words[:], in_=words[0].rearrange("p t r -> p (t r)").bitcast(I32))
+            return pool_words
+
+        def load_scales(scales, queue, name):
+            plane = keep.tile([P, T // 4], I32, name=name)
+            nc.vector.memset(plane[:], 0)
+            rows = scales[0].bitcast(I32)
+            for quad in range(4):
+                queue.dma_start(out=plane[32 * quad : 32 * quad + 4, :], in_=rows[4 * quad : 4 * quad + 4, :])
+            return plane
+
+        def load_by_partition(vec, name):
+            col = keep.tile([P, PACK], F32, name=name)
+            nc.gpsimd.dma_start(out=col[:], in_=vec.rearrange("(p j) -> p j", j=PACK))
+            return col
+
+        def negated(col, name):
+            neg = keep.tile([P, PACK], F32, name=name)
+            nc.gpsimd.tensor_scalar(out=neg[:], in0=col[:], scalar1=-1.0, scalar2=0.0, op0=ALU.mult, op1=ALU.add)
+            return neg
+
+        ks_pool = load_scales(k_scales, nc.scalar, "ks_pool")
+        ls_col = load_by_partition(ls[0, 0, :], "ls_col")
+        cs_pool = load_scales(c_scales, nc.gpsimd, "cs_pool")
+        neg_ls = negated(ls_col, "neg_ls")
+        l2_col = load_by_partition(l2[0, 0, :], "l2_col")
+        lm_col = load_by_partition(lm[0, 0, :], "lm_col")
+        us_col = load_by_partition(us[0, :, 0], "us_col")
+        neg_l2 = negated(l2_col, "neg_l2")
+        neg_lm = negated(lm_col, "neg_lm")
+        ident = keep.tile([P, P], F32, name="ident")
+        make_identity(nc, ident[:])
+        one = keep.tile([P, 1], F32, name="one")
+        nc.gpsimd.memset(one[:], 1.0)
+
+        kw_pool = load_words(k_words, "kw_pool")
+        cw_pool = load_words(c_words, "cw_pool")
+
+        def gather(pool_tile, dtype, name):
+            picked = keep.tile([P, N], dtype, name=name, align_bytes=64)
+            nc.vector.tensor_copy(out=picked[:], in_=pool_tile[:].bitcast(dtype).indirect(offsets[:]))
+            return picked
+
+        ks = gather(ks_pool, U8, "ks")
+
+        q_bf = keep.tile([P, PACK, P, PACK], BF16, name="q_bf", align_bytes=64)
+        q_dst = q_bf[:].rearrange("p i m j -> p m j i")
+        q_src = q_raw[:].rearrange("p j (m i) -> p m j i", i=PACK)
+        half = P // 2
+        nc.scalar.activation(out=q_dst[:, half:], in_=q_src[:, half:], func=ACT.Copy)
+        nc.vector.tensor_copy(out=q_dst[:, :half], in_=q_src[:, :half])
+        q_codes = keep.tile([P, NQ], U32, name="q_codes", align_bytes=64)
+        q_scales = keep.tile([P, NQ], U8, name="q_scales", align_bytes=64)
+        nc.vector.quantize_mx(
+            out=q_codes[:].bitcast(FP8X4), scales=q_scales[:], in_=q_bf[:].rearrange("p i m j -> p (i m j)")
+        )
+
+        kw = gather(kw_pool, U32, "kw")
+
+        def weights(i, words, scales, neg_lse, name):
+            cols = slice(i * P, (i + 1) * P)
+            score = work.tile([P, N], F32, tag="work", name="score")
+            nc.tensor.matmul_mx(
+                out=score[:],
+                lhsT=q_codes[:, cols].bitcast(FP8X4),
+                lhsT_scale=q_scales[:, cols],
+                rhs=words[:].bitcast(FP8X4),
+                rhs_scale=scales[:],
+                start=True,
+                stop=True,
+            )
+            prob = keep.tile([P, PACK, P], F32, name=name)
+            nc.scalar.activation(
+                out=prob[:],
+                in_=score[:].rearrange("p (s t) -> p t s", t=PACK),
+                func=ACT.Exp,
+                bias=neg_lse[:, i : i + 1],
+            )
+            return prob
+
+        first = [weights(i, kw, ks, neg_ls, f"first{i}") for i in range(PACK)]
+        cs = gather(cs_pool, U8, "cs")
+        cw = gather(cw_pool, U32, "cw")
+
+        y_codes = keep.tile([P, NQ], U32, name="y_codes", align_bytes=64)
+        y_scales = keep.tile([P, NQ], U8, name="y_scales", align_bytes=64)
+        v_codes = keep.tile([P, DV], U32, name="v_codes", align_bytes=64)
+        v_scales = keep.tile([P, DV], U8, name="v_scales", align_bytes=64)
+
+        def y_tile(i):
+            cols = slice(i * P, (i + 1) * P)
+            second = weights(i, cw, cs, neg_l2, f"second{i}")
+            taken = ring.tile([P, PACK, P], F32, name="taken")
+            nc.scalar.activation(out=taken[:], in_=second[:], func=ACT.Copy, scale=neg_lm[:, i : i + 1])
+            if i == PACK - 1:
+                warm = keep.tile([P, 1], F32, name="warm")
+                nc.scalar.activation(
+                    out=warm[:], in_=taken[:, 0, 0:1], func=ACT.Abs_reciprocal_sqrt, scale=0.0, bias=one[:]
+                )
+            turned = work.tile([P, PACK, P], F32, tag="work", name="y_turned")
+            for t in range(PACK):
+                nc.tensor.matmul(turned[:, t, :], first[i][:, t, :], ident[:], start=True, stop=False, is_transpose=True)
+                nc.tensor.matmul(turned[:, t, :], taken[:, t, :], ident[:], start=False, stop=True, is_transpose=True)
+            y_bf = ring.tile([P, P, PACK], BF16, name="y_bf", align_bytes=64)
+            nc.vector.tensor_tensor(
+                out=y_bf[:],
+                in0=turned[:].rearrange("p t m -> p m t"),
+                in1=us_col[:].unsqueeze(1).to_broadcast([P, P, PACK]),
+                op=ALU.mult,
+            )
+            nc.vector.quantize_mx(
+                out=y_codes[:, cols].bitcast(FP8X4), scales=y_scales[:, cols], in_=y_bf[:].rearrange("p m t -> p (m t)")
+            )
+
+        def v_block(b):
+            cols = slice(b * P, (b + 1) * P)
+            v_pool = big.tile([P, T], F32, tag="big", name="v_pool")
+            nc.sync.dma_start(out=v_pool[:], in_=vT[cols, :])
+            picked = ring.tile([P, 2, P, 2], BF16, name="v_picked")
+            nc.vector.tensor_copy(out=picked[:].rearrange("p u s r -> p s u r"), in_=v_pool[:].indirect(offsets[:]))
+            pairs = picked[:].rearrange("p u s r -> p u (s r)").bitcast(F32)
+            turned = work.tile([P, 2, P], F32, tag="work", name="v_turned")
+            for u in range(2):
+                nc.tensor.transpose(turned[:, u, :], pairs[:, u, :], ident[:])
+            v_bf = ring.tile([P, P, PACK], BF16, name="v_bf", align_bytes=64)
+            nc.scalar.copy(out=v_bf[:].bitcast(F32), in_=turned[:].rearrange("p u e -> p e u"))
+            nc.vector.quantize_mx(
+                out=v_codes[:, cols].bitcast(FP8X4), scales=v_scales[:, cols], in_=v_bf[:].rearrange("p e t -> p (e t)")
+            )
+
+        sums = [acc.tile([P, DV], F32, name=f"sums{i}") for i in range(PACK)]
+        squares = keep.tile([P, 3, PACK], F32, name="squares")
+
+        def product(i, piece, lo, hi):
+            rows = slice(i * P, (i + 1) * P)
+            nc.tensor.matmul_mx(
+                out=sums[i][:, lo:hi],
+                lhsT=y_codes[:, rows].bitcast(FP8X4),
+                lhsT_scale=y_scales[:, rows],
+                rhs=v_codes[:, lo:hi].bitcast(FP8X4),
+                rhs_scale=v_scales[:, lo:hi],
+                start=True,
+                stop=True,
+            )
+            squared = ring.tile([P, 2 * P], BF16, name="squared")
+            nc.scalar.activation(
+                out=squared[:, : hi - lo], in_=sums[i][:, lo:hi], func=ACT.Square, accum_out=squares[:, piece, i : i + 1]
+            )
+
+        y_tile(0)
+        v_block(0)
+        y_tile(1)
+        y_tile(2)
+        v_block(1)
+        y_tile(3)
+        for i in range(PACK):
+            product(i, 0, 0, 2 * P)
+        v_block(2)
+        for i in range(PACK):
+            product(i, 1, 2 * P, 3 * P)
+        early = keep.tile([P, PACK], F32, name="early")
+        nc.gpsimd.tensor_tensor(out=early[:], in0=squares[:, 0, :], in1=squares[:, 1, :], op=ALU.add)
+        early_eps = keep.tile([P, PACK], F32, name="early_eps")
+        nc.gpsimd.tensor_scalar(out=early_eps[:], in0=early[:], scalar1=1.0 / DV, scalar2=EPS, op0=ALU.mult, op1=ALU.add)
+        v_block(3)
+        rows_out = out[0].rearrange("(m i) e -> m i e", i=PACK)
+        for i in range(PACK):
+            product(i, 2, 3 * P, 4 * P)
+            rstd = keep.tile([P, 1], F32, name=f"rstd{i}")
+            nc.scalar.activation(
+                out=rstd[:],
+                in_=squares[:, 2, i : i + 1],
+                func=ACT.Abs_reciprocal_sqrt,
+                scale=1.0 / DV,
+                bias=early_eps[:, i : i + 1],
+            )
+            result = keep.tile([P, DV], F32, name=f"result{i}")
+            if i < PACK - 1:
+                nc.vector.tensor_scalar(out=result[:], in0=sums[i][:], scalar1=rstd[:], scalar2=None, op0=ALU.mult)
+            else:
+                nc.scalar.activation(out=result[:], in_=sums[i][:], func=ACT.Copy, scale=rstd[:])
+            nc.sync.dma_start(out=rows_out[:, i, :], in_=result[:])

@@ -19,41 +19,60 @@ T = 2048
 N = 512
 NQ = 512
 DV = 512
+HALF = 256
 EPS = 1e-05
 FLOPS = 3 * 2 * 512 * 512 * 512
+TAKE = "XXSS"
+QENG = "BS"
+FIN = "VVSV"
+PIECES = [[0,256],[256,512]]
+FORCE = {1: 0, 2: 3, 3: 2}
 
 
 def tile_attend_at_diff_topk_kernel(tc, qT, k_words, k_scales, c_words, c_scales, vT, ls, lm, l2, us, offs, out):
     nc = tc.nc
     with ExitStack() as ctx:
         keep = ctx.enter_context(tc.tile_pool(name="keep", bufs=1))
-        big = ctx.enter_context(tc.tile_pool(name="big", bufs=3))
-        ring = ctx.enter_context(tc.tile_pool(name="ring", bufs=2))
-        work = ctx.enter_context(tc.psum_pool(name="work", bufs=4))
-        acc = ctx.enter_context(tc.psum_pool(name="acc", bufs=1))
+        r_taken = ctx.enter_context(tc.tile_pool(name="r_taken", bufs=3))
+        r_ybf = ctx.enter_context(tc.tile_pool(name="r_ybf", bufs=3))
+        r_vp = ctx.enter_context(tc.tile_pool(name="r_vp", bufs=4))
+        r_vbf = ctx.enter_context(tc.tile_pool(name="r_vbf", bufs=2))
+        r_sq = ctx.enter_context(tc.tile_pool(name="r_sq", bufs=4))
+        ps_A = ctx.enter_context(tc.psum_pool(name="ps_A", bufs=4))
+        ps_B = ctx.enter_context(tc.psum_pool(name="ps_B", bufs=4))
 
         offsets = keep.tile([P, N // 16], U16, name="offsets")
         nc.sync.dma_start(offsets[:], offs)
 
-        q_raw = big.tile([P, PACK, NQ], F32, tag="big", name="q_raw")
-        nc.sync.dma_start(out=q_raw[:], in_=qT[0].rearrange("(p j) q -> p j q", j=PACK))
+        q_raw, v_pool = {}, {}
 
-        def load_words(words, name):
-            pool_words = big.tile([P, T], I32, tag="big", name=name)
-            nc.sync.dma_start(out=pool_words[:], in_=words[0].rearrange("p t r -> p (t r)").bitcast(I32))
+        def load_q(h, queue):
+            q_raw[h] = keep.tile([P, PACK, HALF], F32, name=f"q_raw{h}")
+            queue.dma_start(out=q_raw[h][:], in_=qT[0][:, h * HALF : (h + 1) * HALF].rearrange("(p j) q -> p j q", j=PACK))
+
+        def load_words(words, name, queue):
+            pool_words = keep.tile([P, T], I32, name=name)
+            queue.dma_start(out=pool_words[:], in_=words[0].rearrange("p t r -> p (t r)").bitcast(I32))
             return pool_words
 
-        def load_scales(scales, queue, name):
+        def zeroed(name):
             plane = keep.tile([P, T // 4], I32, name=name)
             nc.vector.memset(plane[:], 0)
-            rows = scales[0].bitcast(I32)
-            for quad in range(4):
-                queue.dma_start(out=plane[32 * quad : 32 * quad + 4, :], in_=rows[4 * quad : 4 * quad + 4, :])
             return plane
 
-        def load_by_partition(vec, name):
+        def load_quad(plane, scales, quad, queue):
+            rows = scales[0].bitcast(I32)
+            queue.dma_start(out=plane[32 * quad : 32 * quad + 4, :], in_=rows[4 * quad : 4 * quad + 4, :])
+
+        def load_v(b, queue):
+            v_pool[b] = keep.tile([P, T], F32, name=f"v_pool{b}", tag=f"v_pool{b}", align_bytes=64)
+            queue.dma_start(out=v_pool[b][:], in_=vT[b * P : (b + 1) * P, :])
+
+        def load_by_query(vec, name):
             col = keep.tile([P, PACK], F32, name=name)
-            nc.gpsimd.dma_start(out=col[:], in_=vec.rearrange("(p j) -> p j", j=PACK))
+            nc.gpsimd.dma_start(
+                out=col[:].rearrange("p (h i) -> p h i", h=2), in_=vec.rearrange("(h p i) -> p h i", h=2, i=2)
+            )
             return col
 
         def negated(col, name):
@@ -61,13 +80,30 @@ def tile_attend_at_diff_topk_kernel(tc, qT, k_words, k_scales, c_words, c_scales
             nc.gpsimd.tensor_scalar(out=neg[:], in0=col[:], scalar1=-1.0, scalar2=0.0, op0=ALU.mult, op1=ALU.add)
             return neg
 
-        ks_pool = load_scales(k_scales, nc.scalar, "ks_pool")
-        ls_col = load_by_partition(ls[0, 0, :], "ls_col")
-        cs_pool = load_scales(c_scales, nc.gpsimd, "cs_pool")
+        ks_pool = zeroed("ks_pool")
+        cs_pool = zeroed("cs_pool")
+        load_q(0, nc.sync)
+        load_quad(ks_pool, k_scales, 3, nc.sync)
+        load_quad(ks_pool, k_scales, 2, nc.sync)
+        load_quad(ks_pool, k_scales, 0, nc.sync)
+        load_quad(cs_pool, c_scales, 0, nc.sync)
+        load_quad(ks_pool, k_scales, 1, nc.sync)
+        kw_pool = load_words(k_words, "kw_pool", nc.sync)
+        load_quad(cs_pool, c_scales, 1, nc.sync)
+        load_quad(cs_pool, c_scales, 3, nc.sync)
+        load_quad(cs_pool, c_scales, 2, nc.sync)
+        cw_pool = load_words(c_words, "cw_pool", nc.sync)
+        load_q(1, nc.sync)
+        load_v(0, nc.sync)
+        load_v(1, nc.sync)
+        load_v(2, nc.sync)
+        load_v(3, nc.sync)
+        ls_col = load_by_query(ls[0, 0, :], "ls_col")
         neg_ls = negated(ls_col, "neg_ls")
-        l2_col = load_by_partition(l2[0, 0, :], "l2_col")
-        lm_col = load_by_partition(lm[0, 0, :], "lm_col")
-        us_col = load_by_partition(us[0, :, 0], "us_col")
+        l2_col = load_by_query(l2[0, 0, :], "l2_col")
+        lm_col = load_by_query(lm[0, 0, :], "lm_col")
+        us_col = keep.tile([P, PACK], F32, name="us_col")
+        nc.gpsimd.dma_start(out=us_col[:], in_=us[0, :, 0].rearrange("(p j) -> p j", j=PACK))
         neg_l2 = negated(l2_col, "neg_l2")
         neg_lm = negated(lm_col, "neg_lm")
         ident = keep.tile([P, P], F32, name="ident")
@@ -75,33 +111,31 @@ def tile_attend_at_diff_topk_kernel(tc, qT, k_words, k_scales, c_words, c_scales
         one = keep.tile([P, 1], F32, name="one")
         nc.gpsimd.memset(one[:], 1.0)
 
-        kw_pool = load_words(k_words, "kw_pool")
-        cw_pool = load_words(c_words, "cw_pool")
-
         def gather(pool_tile, dtype, name):
             picked = keep.tile([P, N], dtype, name=name, align_bytes=64)
             nc.vector.tensor_copy(out=picked[:], in_=pool_tile[:].bitcast(dtype).indirect(offsets[:]))
             return picked
 
-        ks = gather(ks_pool, U8, "ks")
-
-        q_bf = keep.tile([P, PACK, P, PACK], BF16, name="q_bf", align_bytes=64)
-        q_dst = q_bf[:].rearrange("p i m j -> p m j i")
-        q_src = q_raw[:].rearrange("p j (m i) -> p m j i", i=PACK)
-        half = P // 2
-        nc.scalar.activation(out=q_dst[:, half:], in_=q_src[:, half:], func=ACT.Copy)
-        nc.vector.tensor_copy(out=q_dst[:, :half], in_=q_src[:, :half])
         q_codes = keep.tile([P, NQ], U32, name="q_codes", align_bytes=64)
         q_scales = keep.tile([P, NQ], U8, name="q_scales", align_bytes=64)
-        nc.vector.quantize_mx(
-            out=q_codes[:].bitcast(FP8X4), scales=q_scales[:], in_=q_bf[:].rearrange("p i m j -> p (i m j)")
-        )
 
-        kw = gather(kw_pool, U32, "kw")
+        def q_half(h):
+            q_bf = keep.tile([P, 2, P, PACK], BF16, name=f"q_bf{h}", align_bytes=64)
+            dst = q_bf[:].rearrange("p i m j -> p m j i")
+            src = q_raw[h][:].rearrange("p j (m i) -> p m j i", i=2)
+            cut = {"S": 0, "V": P, "B": P // 2}[QENG[h]]
+            if cut < P:
+                nc.scalar.activation(out=dst[:, cut:], in_=src[:, cut:], func=ACT.Copy)
+            if cut > 0:
+                nc.vector.tensor_copy(out=dst[:, :cut], in_=src[:, :cut])
+            cols = slice(h * HALF, (h + 1) * HALF)
+            nc.vector.quantize_mx(
+                out=q_codes[:, cols].bitcast(FP8X4), scales=q_scales[:, cols], in_=q_bf[:].rearrange("p i m j -> p (i m j)")
+            )
 
         def weights(i, words, scales, neg_lse, name):
             cols = slice(i * P, (i + 1) * P)
-            score = work.tile([P, N], F32, tag="work", name="score")
+            score = ps_A.tile([P, N], F32, tag="bank", name="score")
             nc.tensor.matmul_mx(
                 out=score[:],
                 lhsT=q_codes[:, cols].bitcast(FP8X4),
@@ -120,7 +154,16 @@ def tile_attend_at_diff_topk_kernel(tc, qT, k_words, k_scales, c_words, c_scales
             )
             return prob
 
-        first = [weights(i, kw, ks, neg_ls, f"first{i}") for i in range(PACK)]
+        first, second, taken, y_turned, y_bf, v_picked, v_turned, v_bf, sums = {}, {}, {}, {}, {}, {}, {}, {}, {}
+        ks = gather(ks_pool, U8, "ks")
+        q_half(0)
+        kw = gather(kw_pool, U32, "kw")
+
+        def first_weights(i):
+            first[i] = weights(i, kw, ks, neg_ls, f"first{i}")
+
+        first_weights(0)
+        first_weights(1)
         cs = gather(cs_pool, U8, "cs")
         cw = gather(cw_pool, U32, "cw")
 
@@ -128,97 +171,167 @@ def tile_attend_at_diff_topk_kernel(tc, qT, k_words, k_scales, c_words, c_scales
         y_scales = keep.tile([P, NQ], U8, name="y_scales", align_bytes=64)
         v_codes = keep.tile([P, DV], U32, name="v_codes", align_bytes=64)
         v_scales = keep.tile([P, DV], U8, name="v_scales", align_bytes=64)
+        squares = keep.tile([P, len(PIECES), PACK], F32, name="squares")
+        early_eps = keep.tile([P, PACK], F32, name="early_eps")
 
-        def y_tile(i):
-            cols = slice(i * P, (i + 1) * P)
-            second = weights(i, cw, cs, neg_l2, f"second{i}")
-            taken = ring.tile([P, PACK, P], F32, name="taken")
-            nc.scalar.activation(out=taken[:], in_=second[:], func=ACT.Copy, scale=neg_lm[:, i : i + 1])
-            if i == PACK - 1:
-                warm = keep.tile([P, 1], F32, name="warm")
-                nc.scalar.activation(
-                    out=warm[:], in_=taken[:, 0, 0:1], func=ACT.Abs_reciprocal_sqrt, scale=0.0, bias=one[:]
+        def second_weights(i):
+            second[i] = weights(i, cw, cs, neg_l2, f"second{i}")
+
+        def take(i):
+            taken[i] = r_taken.tile([P, PACK, P], F32, name="taken")
+            factor = neg_lm[:, i : i + 1]
+            if TAKE[i] == "S":
+                nc.scalar.activation(out=taken[i][:], in_=second[i][:], func=ACT.Copy, scale=factor)
+            elif TAKE[i] == "V":
+                nc.vector.tensor_scalar(out=taken[i][:], in0=second[i][:], scalar1=factor, scalar2=None, op0=ALU.mult)
+            else:
+                nc.vector.scalar_tensor_tensor(
+                    out=taken[i][:], in0=second[i][:], scalar=factor, in1=first[i][:], op0=ALU.mult, op1=ALU.add
                 )
-            turned = work.tile([P, PACK, P], F32, tag="work", name="y_turned")
+
+        def warm_up():
+            warm = keep.tile([P, 1], F32, name="warm")
+            nc.scalar.activation(out=warm[:], in_=taken[3][:, 0, 0:1], func=ACT.Abs_reciprocal_sqrt, scale=0.0, bias=last_exp())
+
+        def last_exp():
+            return one[:]
+
+        def turn_y(i):
+            y_turned[i] = ps_B.tile([P, PACK, P], F32, tag="bank", name="y_turned")
             for t in range(PACK):
-                nc.tensor.matmul(turned[:, t, :], first[i][:, t, :], ident[:], start=True, stop=False, is_transpose=True)
-                nc.tensor.matmul(turned[:, t, :], taken[:, t, :], ident[:], start=False, stop=True, is_transpose=True)
-            y_bf = ring.tile([P, P, PACK], BF16, name="y_bf", align_bytes=64)
+                if TAKE[i] == "X":
+                    nc.tensor.transpose(y_turned[i][:, t, :], taken[i][:, t, :], ident[:])
+                else:
+                    nc.tensor.matmul(y_turned[i][:, t, :], first[i][:, t, :], ident[:], start=True, stop=False, is_transpose=True)
+                    nc.tensor.matmul(y_turned[i][:, t, :], taken[i][:, t, :], ident[:], start=False, stop=True, is_transpose=True)
+
+        def round_y(i):
+            if i in FORCE:
+                y_bf[i] = keep.tile([P, P, PACK], BF16, name="y_bf", tag=f"v_pool{FORCE[i]}", align_bytes=64)
+            else:
+                y_bf[i] = r_ybf.tile([P, P, PACK], BF16, name="y_bf", align_bytes=64)
             nc.vector.tensor_tensor(
-                out=y_bf[:],
-                in0=turned[:].rearrange("p t m -> p m t"),
+                out=y_bf[i][:],
+                in0=y_turned[i][:].rearrange("p t m -> p m t"),
                 in1=us_col[:].unsqueeze(1).to_broadcast([P, P, PACK]),
                 op=ALU.mult,
             )
+
+        def quantise_y(i):
+            cols = slice(i * P, (i + 1) * P)
             nc.vector.quantize_mx(
-                out=y_codes[:, cols].bitcast(FP8X4), scales=y_scales[:, cols], in_=y_bf[:].rearrange("p m t -> p (m t)")
+                out=y_codes[:, cols].bitcast(FP8X4), scales=y_scales[:, cols], in_=y_bf[i][:].rearrange("p m t -> p (m t)")
             )
 
-        def v_block(b):
-            cols = slice(b * P, (b + 1) * P)
-            v_pool = big.tile([P, T], F32, tag="big", name="v_pool")
-            nc.sync.dma_start(out=v_pool[:], in_=vT[cols, :])
-            picked = ring.tile([P, 2, P, 2], BF16, name="v_picked")
-            nc.vector.tensor_copy(out=picked[:].rearrange("p u s r -> p s u r"), in_=v_pool[:].indirect(offsets[:]))
-            pairs = picked[:].rearrange("p u s r -> p u (s r)").bitcast(F32)
-            turned = work.tile([P, 2, P], F32, tag="work", name="v_turned")
+        def gather_v(b):
+            v_picked[b] = r_vp.tile([P, 2, P, 2], BF16, name="v_picked")
+            nc.vector.tensor_copy(out=v_picked[b][:].rearrange("p u s r -> p s u r"), in_=v_pool[b][:].indirect(offsets[:]))
+
+        def turn_v(b):
+            pairs = v_picked[b][:].rearrange("p u s r -> p u (s r)").bitcast(F32)
+            v_turned[b] = ps_B.tile([P, 2, P], F32, tag="bank", name="v_turned")
             for u in range(2):
-                nc.tensor.transpose(turned[:, u, :], pairs[:, u, :], ident[:])
-            v_bf = ring.tile([P, P, PACK], BF16, name="v_bf", align_bytes=64)
-            nc.scalar.copy(out=v_bf[:].bitcast(F32), in_=turned[:].rearrange("p u e -> p e u"))
+                nc.tensor.transpose(v_turned[b][:, u, :], pairs[:, u, :], ident[:])
+
+        def copy_v(b):
+            v_bf[b] = r_vbf.tile([P, P, PACK], BF16, name="v_bf", align_bytes=64)
+            nc.scalar.copy(out=v_bf[b][:].bitcast(F32), in_=v_turned[b][:].rearrange("p u e -> p e u"))
+
+        def quantise_v(b):
+            cols = slice(b * P, (b + 1) * P)
             nc.vector.quantize_mx(
-                out=v_codes[:, cols].bitcast(FP8X4), scales=v_scales[:, cols], in_=v_bf[:].rearrange("p e t -> p (e t)")
+                out=v_codes[:, cols].bitcast(FP8X4), scales=v_scales[:, cols], in_=v_bf[b][:].rearrange("p e t -> p (e t)")
             )
 
-        sums = [acc.tile([P, DV], F32, name=f"sums{i}") for i in range(PACK)]
-        squares = keep.tile([P, 3, PACK], F32, name="squares")
-
-        def product(i, piece, lo, hi):
+        def product(i, piece):
+            lo, hi = PIECES[piece]
+            if i not in sums:
+                sums[i] = ps_A.tile([P, DV], F32, tag="bank", name="sums")
             rows = slice(i * P, (i + 1) * P)
-            nc.tensor.matmul_mx(
-                out=sums[i][:, lo:hi],
-                lhsT=y_codes[:, rows].bitcast(FP8X4),
-                lhsT_scale=y_scales[:, rows],
-                rhs=v_codes[:, lo:hi].bitcast(FP8X4),
-                rhs_scale=v_scales[:, lo:hi],
-                start=True,
-                stop=True,
-            )
-            squared = ring.tile([P, 2 * P], BF16, name="squared")
+            for a, b in ((lo, hi),) if hi - lo != 3 * P else ((lo, lo + 2 * P), (lo + 2 * P, hi)):
+                nc.tensor.matmul_mx(
+                    out=sums[i][:, a:b],
+                    lhsT=y_codes[:, rows].bitcast(FP8X4),
+                    lhsT_scale=y_scales[:, rows],
+                    rhs=v_codes[:, a:b].bitcast(FP8X4),
+                    rhs_scale=v_scales[:, a:b],
+                    start=True,
+                    stop=True,
+                )
+            squared = r_sq.tile([P, 3 * P], BF16, name="squared")
             nc.scalar.activation(
                 out=squared[:, : hi - lo], in_=sums[i][:, lo:hi], func=ACT.Square, accum_out=squares[:, piece, i : i + 1]
             )
 
-        y_tile(0)
-        v_block(0)
-        y_tile(1)
-        y_tile(2)
-        v_block(1)
-        y_tile(3)
+        def early_sums():
+            early = squares[:, 0, :]
+            if len(PIECES) > 2:
+                both = keep.tile([P, PACK], F32, name="both")
+                nc.gpsimd.tensor_tensor(out=both[:], in0=squares[:, 0, :], in1=squares[:, 1, :], op=ALU.add)
+                early = both[:]
+            nc.gpsimd.tensor_scalar(out=early_eps[:], in0=early, scalar1=1.0 / DV, scalar2=EPS, op0=ALU.mult, op1=ALU.add)
+
+        gather_v(0)
+        turn_v(0)
+        second_weights(0)
+        take(0)
+        second_weights(1)
+        q_half(1)
+        gather_v(1)
+        gather_v(2)
+        turn_y(0)
+        second_weights(2)
+        take(1)
+        first_weights(2)
+        round_y(0)
+        second_weights(3)
+        take(2)
+        gather_v(3)
+        turn_y(1)
+        round_y(1)
+        turn_y(2)
+        first_weights(3)
+        take(3)
+        copy_v(0)
+        round_y(2)
+        turn_v(1)
+        turn_y(3)
+        turn_v(2)
+        copy_v(1)
+        quantise_v(0)
+        quantise_y(0)
+        round_y(3)
+        quantise_y(1)
+        quantise_y(2)
+        quantise_y(3)
+        quantise_v(1)
+        product(3, 0)
+        product(2, 0)
+        product(1, 0)
+        product(0, 0)
+        early_sums()
+        copy_v(2)
+        turn_v(3)
+        warm_up()
+        copy_v(3)
+        quantise_v(2)
+        quantise_v(3)
+
+        last = len(PIECES) - 1
+        rows_out = out[0].rearrange("(h m i) e -> m h i e", h=2, i=2)
         for i in range(PACK):
-            product(i, 0, 0, 2 * P)
-        v_block(2)
-        for i in range(PACK):
-            product(i, 1, 2 * P, 3 * P)
-        early = keep.tile([P, PACK], F32, name="early")
-        nc.gpsimd.tensor_tensor(out=early[:], in0=squares[:, 0, :], in1=squares[:, 1, :], op=ALU.add)
-        early_eps = keep.tile([P, PACK], F32, name="early_eps")
-        nc.gpsimd.tensor_scalar(out=early_eps[:], in0=early[:], scalar1=1.0 / DV, scalar2=EPS, op0=ALU.mult, op1=ALU.add)
-        v_block(3)
-        rows_out = out[0].rearrange("(m i) e -> m i e", i=PACK)
-        for i in range(PACK):
-            product(i, 2, 3 * P, 4 * P)
+            product(i, last)
             rstd = keep.tile([P, 1], F32, name=f"rstd{i}")
             nc.scalar.activation(
                 out=rstd[:],
-                in_=squares[:, 2, i : i + 1],
+                in_=squares[:, last, i : i + 1],
                 func=ACT.Abs_reciprocal_sqrt,
                 scale=1.0 / DV,
                 bias=early_eps[:, i : i + 1],
             )
             result = keep.tile([P, DV], F32, name=f"result{i}")
-            if i < PACK - 1:
+            if FIN[i] == "V":
                 nc.vector.tensor_scalar(out=result[:], in0=sums[i][:], scalar1=rstd[:], scalar2=None, op0=ALU.mult)
             else:
                 nc.scalar.activation(out=result[:], in_=sums[i][:], func=ACT.Copy, scale=rstd[:])
-            nc.sync.dma_start(out=rows_out[:, i, :], in_=result[:])
+            nc.sync.dma_start(out=rows_out[:, i // 2, i % 2, :], in_=result[:])

@@ -15,201 +15,179 @@ ALU = mybir.AluOpType
 
 P = 128
 PACK = 4
-T = 2048
-N = 512
-NQ = 512
+TOKENS = 2048
+SLOTS = 512
+QUERIES = 512
 DV = 512
+TILES = QUERIES // P
+BLOCKS = DV // P
 HALF = 256
+SCALE_ROWS = 16
+C_ROW0 = 4
+SPLIT_TILES = 2
 EPS = 1e-05
-FLOPS = 3 * 2 * 512 * 512 * 512
-TAKE = "XXSS"
-QENG = "BS"
-FIN = "VVSV"
-PIECES = [[0,256],[256,512]]
-FORCE = {1: 0, 2: 3, 3: 2}
+FLOPS = 3 * 2 * 512 * SLOTS * QUERIES
+
+BUFFER_OF = {
+    "second2": "second0",
+    "second3": "second1",
+    "v_bf0": "second3",
+    "y_bf0": "v_pool1",
+    "y_bf1": "v_pool2",
+    "v_words0": "v_pool3",
+    "y_words1": "v_bf0",
+    "y_bf2": "v_picked3",
+    "y_bf3": "v_bf1",
+}
+
+
+def buffer_tag(name):
+    return buffer_tag(BUFFER_OF[name]) if name in BUFFER_OF else name
 
 
 def tile_attend_at_diff_topk_kernel(tc, qT, k_words, k_scales, c_words, c_scales, vT, ls, lm, l2, us, offs, out):
     nc = tc.nc
     with ExitStack() as ctx:
-        keep = ctx.enter_context(tc.tile_pool(name="keep", bufs=1))
-        r_taken = ctx.enter_context(tc.tile_pool(name="r_taken", bufs=3))
-        r_ybf = ctx.enter_context(tc.tile_pool(name="r_ybf", bufs=3))
-        r_vp = ctx.enter_context(tc.tile_pool(name="r_vp", bufs=4))
-        r_vbf = ctx.enter_context(tc.tile_pool(name="r_vbf", bufs=2))
-        r_sq = ctx.enter_context(tc.tile_pool(name="r_sq", bufs=4))
-        ps_A = ctx.enter_context(tc.psum_pool(name="ps_A", bufs=4))
-        ps_B = ctx.enter_context(tc.psum_pool(name="ps_B", bufs=4))
+        sbuf = ctx.enter_context(tc.tile_pool(name="sbuf", bufs=1))
+        tile_banks = ctx.enter_context(tc.psum_pool(name="tile_banks", bufs=1))
+        value_banks = ctx.enter_context(tc.psum_pool(name="value_banks", bufs=BLOCKS))
 
-        offsets = keep.tile([P, N // 16], U16, name="offsets")
+        def new(name, shape, dtype):
+            return sbuf.tile(shape, dtype, name=name, tag=buffer_tag(name), align_bytes=64)
+
+        def bank(i, shape):
+            return tile_banks.tile(shape, F32, name="bank", tag=f"bank{i}")
+
+        offsets = sbuf.tile([P, SLOTS // 16], U16, name="offsets")
         nc.sync.dma_start(offsets[:], offs)
 
-        q_raw, v_pool = {}, {}
+        def load_queries(h):
+            raw = new(f"q_raw{h}", [P, PACK, HALF], F32)
+            nc.sync.dma_start(out=raw[:], in_=qT[0][:, h * HALF : (h + 1) * HALF].rearrange("(p j) q -> p j q", j=PACK))
+            return raw
 
-        def load_q(h, queue):
-            q_raw[h] = keep.tile([P, PACK, HALF], F32, name=f"q_raw{h}")
-            queue.dma_start(out=q_raw[h][:], in_=qT[0][:, h * HALF : (h + 1) * HALF].rearrange("(p j) q -> p j q", j=PACK))
+        def load_words(words, name):
+            pool = new(name, [P, TOKENS], I32)
+            nc.sync.dma_start(out=pool[:], in_=words[0].rearrange("p t r -> p (t r)").bitcast(I32))
+            return pool
 
-        def load_words(words, name, queue):
-            pool_words = keep.tile([P, T], I32, name=name)
-            queue.dma_start(out=pool_words[:], in_=words[0].rearrange("p t r -> p (t r)").bitcast(I32))
-            return pool_words
+        def zeroed_scale_pool(name):
+            pool = new(name, [P, TOKENS // 4], I32)
+            nc.vector.memset(pool[:], 0)
+            return pool
 
-        def zeroed(name):
-            plane = keep.tile([P, T // 4], I32, name=name)
-            nc.vector.memset(plane[:], 0)
-            return plane
-
-        def load_quad(plane, scales, quad, queue):
+        def load_scales(pool, scales, row0):
             rows = scales[0].bitcast(I32)
-            queue.dma_start(out=plane[32 * quad : 32 * quad + 4, :], in_=rows[4 * quad : 4 * quad + 4, :])
+            for r in range(4):
+                nc.sync.dma_start(out=pool[row0 + r : P : 32, :], in_=rows[r:SCALE_ROWS:4, :])
 
-        def load_v(b, queue):
-            v_pool[b] = keep.tile([P, T], F32, name=f"v_pool{b}", tag=f"v_pool{b}", align_bytes=64)
-            queue.dma_start(out=v_pool[b][:], in_=vT[b * P : (b + 1) * P, :])
-
-        def load_by_query(vec, name):
-            col = keep.tile([P, PACK], F32, name=name)
-            nc.gpsimd.dma_start(
-                out=col[:].rearrange("p (h i) -> p h i", h=2), in_=vec.rearrange("(h p i) -> p h i", h=2, i=2)
-            )
+        def load_by_query(vec, name, queue):
+            col = new(name, [P, TILES], F32)
+            queue.dma_start(out=col[:].rearrange("p (h r) -> p h r", h=2), in_=vec.rearrange("(h p r) -> p h r", h=2, r=2))
             return col
 
+        def load_values(b):
+            pool = new(f"v_pool{b}", [P, TOKENS], F32)
+            nc.sync.dma_start(out=pool[:], in_=vT[b * P : (b + 1) * P, :])
+            return pool
+
         def negated(col, name):
-            neg = keep.tile([P, PACK], F32, name=name)
+            neg = new(name, [P, TILES], F32)
             nc.gpsimd.tensor_scalar(out=neg[:], in0=col[:], scalar1=-1.0, scalar2=0.0, op0=ALU.mult, op1=ALU.add)
             return neg
 
-        ks_pool = zeroed("ks_pool")
-        cs_pool = zeroed("cs_pool")
-        load_q(0, nc.sync)
-        load_quad(ks_pool, k_scales, 3, nc.sync)
-        load_quad(ks_pool, k_scales, 2, nc.sync)
-        load_quad(ks_pool, k_scales, 0, nc.sync)
-        load_quad(cs_pool, c_scales, 0, nc.sync)
-        load_quad(ks_pool, k_scales, 1, nc.sync)
-        kw_pool = load_words(k_words, "kw_pool", nc.sync)
-        load_quad(cs_pool, c_scales, 1, nc.sync)
-        load_quad(cs_pool, c_scales, 3, nc.sync)
-        load_quad(cs_pool, c_scales, 2, nc.sync)
-        cw_pool = load_words(c_words, "cw_pool", nc.sync)
-        load_q(1, nc.sync)
-        load_v(0, nc.sync)
-        load_v(1, nc.sync)
-        load_v(2, nc.sync)
-        load_v(3, nc.sync)
-        ls_col = load_by_query(ls[0, 0, :], "ls_col")
+        ks_pool = zeroed_scale_pool("ks_pool")
+        cs_pool = zeroed_scale_pool("cs_pool")
+        ls_col = load_by_query(ls[0, 0, :], "ls_col", nc.gpsimd)
+        l2_col = load_by_query(l2[0, 0, :], "l2_col", nc.gpsimd)
+        us_col = new("us_col", [P, PACK], F32)
+        nc.gpsimd.dma_start(out=us_col[:], in_=us[0, :, 0].rearrange("(p t) -> p t", t=PACK))
+        q_raw = [load_queries(0)]
+        load_scales(ks_pool, k_scales, 0)
+        q_raw.append(load_queries(1))
+        kw_pool = load_words(k_words, "kw_pool")
+        load_scales(cs_pool, c_scales, C_ROW0)
+        lm_col = load_by_query(lm[0, 0, :], "lm_col", nc.sync)
+        cw_pool = load_words(c_words, "cw_pool")
+        v_pool = [load_values(b) for b in range(BLOCKS)]
+
+        ident = new("ident", [P, P], F32)
+        make_identity(nc, ident[:])
+        one = new("one", [P, 1], F32)
+        nc.gpsimd.memset(one[:], 1.0)
+        eps = new("eps", [P, 1], F32)
+        nc.gpsimd.tensor_scalar(out=eps[:], in0=one[:], scalar1=EPS, scalar2=0.0, op0=ALU.mult, op1=ALU.add)
         neg_ls = negated(ls_col, "neg_ls")
-        l2_col = load_by_query(l2[0, 0, :], "l2_col")
-        lm_col = load_by_query(lm[0, 0, :], "lm_col")
-        us_col = keep.tile([P, PACK], F32, name="us_col")
-        nc.gpsimd.dma_start(out=us_col[:], in_=us[0, :, 0].rearrange("(p j) -> p j", j=PACK))
         neg_l2 = negated(l2_col, "neg_l2")
         neg_lm = negated(lm_col, "neg_lm")
-        ident = keep.tile([P, P], F32, name="ident")
-        make_identity(nc, ident[:])
-        one = keep.tile([P, 1], F32, name="one")
-        nc.gpsimd.memset(one[:], 1.0)
 
-        def gather(pool_tile, dtype, name):
-            picked = keep.tile([P, N], dtype, name=name, align_bytes=64)
-            nc.vector.tensor_copy(out=picked[:], in_=pool_tile[:].bitcast(dtype).indirect(offsets[:]))
+        q_words = new("q_words", [P, QUERIES], U32)
+        q_scales = new("q_scales", [P, QUERIES], U8)
+        squares = new("squares", [P, 2, TILES], F32)
+        early = new("early", [P, SPLIT_TILES], F32)
+        first, second, taken, y_turned, y_bf, y_words, y_scales, sums = {}, {}, {}, {}, {}, {}, {}, {}
+        v_picked, v_turned, v_bf, v_words, v_scales = {}, {}, {}, {}, {}
+
+        def gather_packed(pool, dtype, name):
+            picked = new(name, [P, SLOTS], dtype)
+            nc.vector.tensor_copy(out=picked[:], in_=pool[:].bitcast(dtype).indirect(offsets[:]))
             return picked
 
-        q_codes = keep.tile([P, NQ], U32, name="q_codes", align_bytes=64)
-        q_scales = keep.tile([P, NQ], U8, name="q_scales", align_bytes=64)
-
-        def q_half(h):
-            q_bf = keep.tile([P, 2, P, PACK], BF16, name=f"q_bf{h}", align_bytes=64)
-            dst = q_bf[:].rearrange("p i m j -> p m j i")
-            src = q_raw[h][:].rearrange("p j (m i) -> p m j i", i=2)
-            cut = {"S": 0, "V": P, "B": P // 2}[QENG[h]]
-            if cut < P:
-                nc.scalar.activation(out=dst[:, cut:], in_=src[:, cut:], func=ACT.Copy)
-            if cut > 0:
-                nc.vector.tensor_copy(out=dst[:, :cut], in_=src[:, :cut])
+        def quantise_queries(h):
+            q_bf = new(f"q_bf{h}", [P, 2, P, PACK], BF16)
+            nc.scalar.activation(
+                out=q_bf[:].rearrange("p r m j -> p m j r"),
+                in_=q_raw[h][:].rearrange("p j (m r) -> p m j r", r=2),
+                func=ACT.Copy,
+            )
             cols = slice(h * HALF, (h + 1) * HALF)
             nc.vector.quantize_mx(
-                out=q_codes[:, cols].bitcast(FP8X4), scales=q_scales[:, cols], in_=q_bf[:].rearrange("p i m j -> p (i m j)")
+                out=q_words[:, cols].bitcast(FP8X4), scales=q_scales[:, cols], in_=q_bf[:].rearrange("p r m j -> p (r m j)")
             )
 
-        def weights(i, words, scales, neg_lse, name):
+        def exp_scores(i, words, scales, neg_lse, name):
             cols = slice(i * P, (i + 1) * P)
-            score = ps_A.tile([P, N], F32, tag="bank", name="score")
+            score = bank(i, [P, SLOTS])
             nc.tensor.matmul_mx(
                 out=score[:],
-                lhsT=q_codes[:, cols].bitcast(FP8X4),
+                lhsT=q_words[:, cols].bitcast(FP8X4),
                 lhsT_scale=q_scales[:, cols],
                 rhs=words[:].bitcast(FP8X4),
-                rhs_scale=scales[:],
+                rhs_scale=scales,
                 start=True,
                 stop=True,
             )
-            prob = keep.tile([P, PACK, P], F32, name=name)
+            weights = new(name, [P, PACK, P], F32)
             nc.scalar.activation(
-                out=prob[:],
+                out=weights[:],
                 in_=score[:].rearrange("p (s t) -> p t s", t=PACK),
                 func=ACT.Exp,
                 bias=neg_lse[:, i : i + 1],
             )
-            return prob
-
-        first, second, taken, y_turned, y_bf, v_picked, v_turned, v_bf, sums = {}, {}, {}, {}, {}, {}, {}, {}, {}
-        ks = gather(ks_pool, U8, "ks")
-        q_half(0)
-        kw = gather(kw_pool, U32, "kw")
+            return weights
 
         def first_weights(i):
-            first[i] = weights(i, kw, ks, neg_ls, f"first{i}")
-
-        first_weights(0)
-        first_weights(1)
-        cs = gather(cs_pool, U8, "cs")
-        cw = gather(cw_pool, U32, "cw")
-
-        y_codes = keep.tile([P, NQ], U32, name="y_codes", align_bytes=64)
-        y_scales = keep.tile([P, NQ], U8, name="y_scales", align_bytes=64)
-        v_codes = keep.tile([P, DV], U32, name="v_codes", align_bytes=64)
-        v_scales = keep.tile([P, DV], U8, name="v_scales", align_bytes=64)
-        squares = keep.tile([P, len(PIECES), PACK], F32, name="squares")
-        early_eps = keep.tile([P, PACK], F32, name="early_eps")
+            first[i] = exp_scores(i, kw, ks[:], neg_ls, f"first{i}")
 
         def second_weights(i):
-            second[i] = weights(i, cw, cs, neg_l2, f"second{i}")
+            second[i] = exp_scores(i, cw, cs[C_ROW0:P, :], neg_l2, f"second{i}")
 
         def take(i):
-            taken[i] = r_taken.tile([P, PACK, P], F32, name="taken")
-            factor = neg_lm[:, i : i + 1]
-            if TAKE[i] == "S":
-                nc.scalar.activation(out=taken[i][:], in_=second[i][:], func=ACT.Copy, scale=factor)
-            elif TAKE[i] == "V":
-                nc.vector.tensor_scalar(out=taken[i][:], in0=second[i][:], scalar1=factor, scalar2=None, op0=ALU.mult)
+            taken[i] = new(f"taken{i}", [P, PACK, P], F32)
+            nc.scalar.activation(out=taken[i][:], in_=second[i][:], func=ACT.Copy, scale=neg_lm[:, i : i + 1])
+
+        def turn_weights(i):
+            y_turned[i] = bank(i, [P, PACK, P])
+            if i == 0:
+                passes = [(first[i], t, t == 0, False) for t in range(PACK)]
+                passes += [(taken[i], t, False, t == PACK - 1) for t in range(PACK)]
             else:
-                nc.vector.scalar_tensor_tensor(
-                    out=taken[i][:], in0=second[i][:], scalar=factor, in1=first[i][:], op0=ALU.mult, op1=ALU.add
-                )
+                passes = [(src, t, src is first[i], src is taken[i]) for t in range(PACK) for src in (first[i], taken[i])]
+            for src, t, start, stop in passes:
+                nc.tensor.matmul(y_turned[i][:, t, :], src[:, t, :], ident[:], start=start, stop=stop, is_transpose=True)
 
-        def warm_up():
-            warm = keep.tile([P, 1], F32, name="warm")
-            nc.scalar.activation(out=warm[:], in_=taken[3][:, 0, 0:1], func=ACT.Abs_reciprocal_sqrt, scale=0.0, bias=last_exp())
-
-        def last_exp():
-            return one[:]
-
-        def turn_y(i):
-            y_turned[i] = ps_B.tile([P, PACK, P], F32, tag="bank", name="y_turned")
-            for t in range(PACK):
-                if TAKE[i] == "X":
-                    nc.tensor.transpose(y_turned[i][:, t, :], taken[i][:, t, :], ident[:])
-                else:
-                    nc.tensor.matmul(y_turned[i][:, t, :], first[i][:, t, :], ident[:], start=True, stop=False, is_transpose=True)
-                    nc.tensor.matmul(y_turned[i][:, t, :], taken[i][:, t, :], ident[:], start=False, stop=True, is_transpose=True)
-
-        def round_y(i):
-            if i in FORCE:
-                y_bf[i] = keep.tile([P, P, PACK], BF16, name="y_bf", tag=f"v_pool{FORCE[i]}", align_bytes=64)
-            else:
-                y_bf[i] = r_ybf.tile([P, P, PACK], BF16, name="y_bf", align_bytes=64)
+        def round_weights(i):
+            y_bf[i] = new(f"y_bf{i}", [P, P, PACK], BF16)
             nc.vector.tensor_tensor(
                 out=y_bf[i][:],
                 in0=y_turned[i][:].rearrange("p t m -> p m t"),
@@ -217,120 +195,120 @@ def tile_attend_at_diff_topk_kernel(tc, qT, k_words, k_scales, c_words, c_scales
                 op=ALU.mult,
             )
 
-        def quantise_y(i):
-            cols = slice(i * P, (i + 1) * P)
+        def quantise_weights(i):
+            y_words[i] = new(f"y_words{i}", [P, P], U32)
+            y_scales[i] = new(f"y_scales{i}", [P, P], U8)
             nc.vector.quantize_mx(
-                out=y_codes[:, cols].bitcast(FP8X4), scales=y_scales[:, cols], in_=y_bf[i][:].rearrange("p m t -> p (m t)")
+                out=y_words[i][:].bitcast(FP8X4), scales=y_scales[i][:], in_=y_bf[i][:].rearrange("p m t -> p (m t)")
             )
 
-        def gather_v(b):
-            v_picked[b] = r_vp.tile([P, 2, P, 2], BF16, name="v_picked")
+        def gather_values(b):
+            v_picked[b] = new(f"v_picked{b}", [P, 2, P, 2], BF16)
             nc.vector.tensor_copy(out=v_picked[b][:].rearrange("p u s r -> p s u r"), in_=v_pool[b][:].indirect(offsets[:]))
 
-        def turn_v(b):
+        def turn_values(b):
             pairs = v_picked[b][:].rearrange("p u s r -> p u (s r)").bitcast(F32)
-            v_turned[b] = ps_B.tile([P, 2, P], F32, tag="bank", name="v_turned")
+            v_turned[b] = value_banks.tile([P, 2, P], F32, name="v_turned")
             for u in range(2):
                 nc.tensor.transpose(v_turned[b][:, u, :], pairs[:, u, :], ident[:])
 
-        def copy_v(b):
-            v_bf[b] = r_vbf.tile([P, P, PACK], BF16, name="v_bf", align_bytes=64)
-            nc.scalar.copy(out=v_bf[b][:].bitcast(F32), in_=v_turned[b][:].rearrange("p u e -> p e u"))
+        def copy_values(h):
+            v_bf[h] = new(f"v_bf{h}", [P, 2, P, PACK], BF16)
+            for k in range(2):
+                nc.scalar.copy(out=v_bf[h][:, k].bitcast(F32), in_=v_turned[2 * h + k][:].rearrange("p u e -> p e u"))
 
-        def quantise_v(b):
-            cols = slice(b * P, (b + 1) * P)
+        def quantise_values(h):
+            v_words[h] = new(f"v_words{h}", [P, HALF], U32)
+            v_scales[h] = new(f"v_scales{h}", [P, HALF], U8)
             nc.vector.quantize_mx(
-                out=v_codes[:, cols].bitcast(FP8X4), scales=v_scales[:, cols], in_=v_bf[b][:].rearrange("p e t -> p (e t)")
+                out=v_words[h][:].bitcast(FP8X4), scales=v_scales[h][:], in_=v_bf[h][:].rearrange("p k e t -> p (k e t)")
             )
 
-        def product(i, piece):
-            lo, hi = PIECES[piece]
-            if i not in sums:
-                sums[i] = ps_A.tile([P, DV], F32, tag="bank", name="sums")
-            rows = slice(i * P, (i + 1) * P)
-            for a, b in ((lo, hi),) if hi - lo != 3 * P else ((lo, lo + 2 * P), (lo + 2 * P, hi)):
+        def load_rsqrt_table():
+            warm = new("warm", [P, 1], F32)
+            nc.scalar.activation(
+                out=warm[:], in_=v_bf[0][:, 1, 0, 0:1], func=ACT.Abs_reciprocal_sqrt, scale=taken[TILES - 1][:, 0, 0:1], bias=one[:]
+            )
+
+        def product(i, halves):
+            if halves[0] == 0:
+                sums[i] = bank(i, [P, DV])
+            for h in halves:
                 nc.tensor.matmul_mx(
-                    out=sums[i][:, a:b],
-                    lhsT=y_codes[:, rows].bitcast(FP8X4),
-                    lhsT_scale=y_scales[:, rows],
-                    rhs=v_codes[:, a:b].bitcast(FP8X4),
-                    rhs_scale=v_scales[:, a:b],
+                    out=sums[i][:, h * HALF : (h + 1) * HALF],
+                    lhsT=y_words[i][:].bitcast(FP8X4),
+                    lhsT_scale=y_scales[i][:],
+                    rhs=v_words[h][:].bitcast(FP8X4),
+                    rhs_scale=v_scales[h][:],
                     start=True,
                     stop=True,
                 )
-            squared = r_sq.tile([P, 3 * P], BF16, name="squared")
+            squared = new(f"squared{i}_{halves[-1]}", [P, len(halves) * HALF], BF16)
             nc.scalar.activation(
-                out=squared[:, : hi - lo], in_=sums[i][:, lo:hi], func=ACT.Square, accum_out=squares[:, piece, i : i + 1]
+                out=squared[:],
+                in_=sums[i][:, halves[0] * HALF : (halves[-1] + 1) * HALF],
+                func=ACT.Square,
+                accum_out=squares[:, halves[-1], i : i + 1],
             )
 
-        def early_sums():
-            early = squares[:, 0, :]
-            if len(PIECES) > 2:
-                both = keep.tile([P, PACK], F32, name="both")
-                nc.gpsimd.tensor_tensor(out=both[:], in0=squares[:, 0, :], in1=squares[:, 1, :], op=ALU.add)
-                early = both[:]
-            nc.gpsimd.tensor_scalar(out=early_eps[:], in0=early, scalar1=1.0 / DV, scalar2=EPS, op0=ALU.mult, op1=ALU.add)
-
-        gather_v(0)
-        turn_v(0)
-        second_weights(0)
-        take(0)
-        second_weights(1)
-        q_half(1)
-        gather_v(1)
-        gather_v(2)
-        turn_y(0)
-        second_weights(2)
-        take(1)
+        ks = gather_packed(ks_pool, U8, "ks")
+        quantise_queries(0)
+        kw = gather_packed(kw_pool, U32, "kw")
+        first_weights(0)
+        first_weights(1)
+        cs = gather_packed(cs_pool, U8, "cs")
+        cw = gather_packed(cw_pool, U32, "cw")
+        quantise_queries(1)
         first_weights(2)
-        round_y(0)
-        second_weights(3)
-        take(2)
-        gather_v(3)
-        turn_y(1)
-        round_y(1)
-        turn_y(2)
         first_weights(3)
-        take(3)
-        copy_v(0)
-        round_y(2)
-        turn_v(1)
-        turn_y(3)
-        turn_v(2)
-        copy_v(1)
-        quantise_v(0)
-        quantise_y(0)
-        round_y(3)
-        quantise_y(1)
-        quantise_y(2)
-        quantise_y(3)
-        quantise_v(1)
-        product(3, 0)
-        product(2, 0)
-        product(1, 0)
-        product(0, 0)
-        early_sums()
-        copy_v(2)
-        turn_v(3)
-        warm_up()
-        copy_v(3)
-        quantise_v(2)
-        quantise_v(3)
 
-        last = len(PIECES) - 1
-        rows_out = out[0].rearrange("(h m i) e -> m h i e", h=2, i=2)
-        for i in range(PACK):
-            product(i, last)
-            rstd = keep.tile([P, 1], F32, name=f"rstd{i}")
+        for step in (second_weights, take, turn_weights, gather_values):
+            step(0)
+            step(1)
+        for step in (second_weights, take):
+            step(2)
+            step(3)
+        turn_values(0)
+        turn_values(1)
+        copy_values(0)
+        load_rsqrt_table()
+        round_weights(0)
+        quantise_weights(0)
+        turn_weights(2)
+        turn_weights(3)
+        gather_values(2)
+        turn_values(2)
+        round_weights(1)
+        gather_values(3)
+        turn_values(3)
+        quantise_values(0)
+        quantise_weights(1)
+        copy_values(1)
+        for i in range(SPLIT_TILES):
+            product(i, [0])
+        nc.gpsimd.tensor_scalar(
+            out=early[:], in0=squares[:, 0, :SPLIT_TILES], scalar1=1.0 / DV, scalar2=EPS, op0=ALU.mult, op1=ALU.add
+        )
+        round_weights(2)
+        quantise_values(1)
+        quantise_weights(2)
+        round_weights(3)
+        quantise_weights(3)
+
+        rows_out = out[0].rearrange("(h m r) e -> m h r e", h=2, r=2)
+        for i in range(TILES):
+            split = i < SPLIT_TILES
+            product(i, [1] if split else [0, 1])
+            rstd = new(f"rstd{i}", [P, 1], F32)
             nc.scalar.activation(
                 out=rstd[:],
-                in_=squares[:, last, i : i + 1],
+                in_=squares[:, 1, i : i + 1],
                 func=ACT.Abs_reciprocal_sqrt,
                 scale=1.0 / DV,
-                bias=early_eps[:, i : i + 1],
+                bias=early[:, i : i + 1] if split else eps[:],
             )
-            result = keep.tile([P, DV], F32, name=f"result{i}")
-            if FIN[i] == "V":
+            result = new(f"result{i}", [P, DV], F32)
+            if i < TILES - 1:
                 nc.vector.tensor_scalar(out=result[:], in0=sums[i][:], scalar1=rstd[:], scalar2=None, op0=ALU.mult)
             else:
                 nc.scalar.activation(out=result[:], in_=sums[i][:], func=ACT.Copy, scale=rstd[:])

@@ -24,107 +24,101 @@ BLOCKS = DV // P
 HALF = 256
 SCALE_ROWS = 16
 C_ROW0 = 4
-SPLIT_TILES = 2
 EPS = 1e-05
 FLOPS = 3 * 2 * 512 * SLOTS * QUERIES
 
-BUFFER_OF = {
-    "second2": "second0",
-    "second3": "second1",
-    "v_bf0": "second3",
-    "y_bf0": "v_pool1",
-    "y_bf1": "v_pool2",
-    "v_words0": "v_pool3",
-    "y_words1": "v_bf0",
-    "y_bf2": "v_picked3",
-    "y_bf3": "v_bf1",
+VECTOR_ROWS = 84
+A_BANK = (0, 1, 2, 3)
+Z_BANK = (4, 5, 2, 3)
+Y_BANK = (0, 1, 4, 5)
+SPLIT_TILES = 2
+POOL_BYTES = TOKENS * 4
+
+AFTER_GATHER = {
+    "y_bf0": (1, 0),
+    "y_bf1": (1, 1024),
+    "y_words1": (2, 0),
+    "v_words0": (2, 2048),
+    "y_bf2": (3, 0),
+    "v_words1": (3, 2048),
+    "v_bf3": (3, 4096),
+    "y_bf3": (3, 4096),
 }
-
-
-def buffer_tag(name):
-    return buffer_tag(BUFFER_OF[name]) if name in BUFFER_OF else name
 
 
 def tile_attend_at_diff_topk_kernel(tc, qT, k_words, k_scales, c_words, c_scales, vT, ls, lm, l2, us, offs, out):
     nc = tc.nc
     with ExitStack() as ctx:
         sbuf = ctx.enter_context(tc.tile_pool(name="sbuf", bufs=1))
+        relay = ctx.enter_context(tc.tile_pool(name="relay", bufs=1))
         tile_banks = ctx.enter_context(tc.psum_pool(name="tile_banks", bufs=1))
-        value_banks = ctx.enter_context(tc.psum_pool(name="value_banks", bufs=BLOCKS))
+        value_banks = ctx.enter_context(tc.psum_pool(name="value_banks", bufs=2))
 
         def new(name, shape, dtype):
-            return sbuf.tile(shape, dtype, name=name, tag=buffer_tag(name), align_bytes=64)
+            if name in AFTER_GATHER:
+                block, start = AFTER_GATHER[name]
+                return relay.tile(shape, dtype, name=name, align_bytes=64, offset=block * POOL_BYTES + start)
+            return sbuf.tile(shape, dtype, name=name, align_bytes=64)
 
         def bank(i, shape):
             return tile_banks.tile(shape, F32, name="bank", tag=f"bank{i}")
-
-        offsets = sbuf.tile([P, SLOTS // 16], U16, name="offsets")
-        nc.sync.dma_start(offsets[:], offs)
-
-        def load_queries(h):
-            raw = new(f"q_raw{h}", [P, PACK, HALF], F32)
-            nc.sync.dma_start(out=raw[:], in_=qT[0][:, h * HALF : (h + 1) * HALF].rearrange("(p j) q -> p j q", j=PACK))
-            return raw
 
         def load_words(words, name):
             pool = new(name, [P, TOKENS], I32)
             nc.sync.dma_start(out=pool[:], in_=words[0].rearrange("p t r -> p (t r)").bitcast(I32))
             return pool
 
-        def zeroed_scale_pool(name):
+        def load_scales(scales, row0, name):
             pool = new(name, [P, TOKENS // 4], I32)
             nc.vector.memset(pool[:], 0)
-            return pool
-
-        def load_scales(pool, scales, row0):
             rows = scales[0].bitcast(I32)
             for r in range(4):
                 nc.sync.dma_start(out=pool[row0 + r : P : 32, :], in_=rows[r:SCALE_ROWS:4, :])
-
-        def load_by_query(vec, name, queue):
-            col = new(name, [P, TILES], F32)
-            queue.dma_start(out=col[:].rearrange("p (h r) -> p h r", h=2), in_=vec.rearrange("(h p r) -> p h r", h=2, r=2))
-            return col
-
-        def load_values(b):
-            pool = new(f"v_pool{b}", [P, TOKENS], F32)
-            nc.sync.dma_start(out=pool[:], in_=vT[b * P : (b + 1) * P, :])
             return pool
+
+        def load_columns(vec, name, queue):
+            col = new(name, [P, PACK], F32)
+            queue.dma_start(out=col[:], in_=vec.rearrange("(p t) -> p t", t=PACK))
+            return col
 
         def negated(col, name):
             neg = new(name, [P, TILES], F32)
             nc.gpsimd.tensor_scalar(out=neg[:], in0=col[:], scalar1=-1.0, scalar2=0.0, op0=ALU.mult, op1=ALU.add)
             return neg
 
-        ks_pool = zeroed_scale_pool("ks_pool")
-        cs_pool = zeroed_scale_pool("cs_pool")
-        ls_col = load_by_query(ls[0, 0, :], "ls_col", nc.gpsimd)
-        l2_col = load_by_query(l2[0, 0, :], "l2_col", nc.gpsimd)
-        us_col = new("us_col", [P, PACK], F32)
-        nc.gpsimd.dma_start(out=us_col[:], in_=us[0, :, 0].rearrange("(p t) -> p t", t=PACK))
-        q_raw = [load_queries(0)]
-        load_scales(ks_pool, k_scales, 0)
-        q_raw.append(load_queries(1))
-        kw_pool = load_words(k_words, "kw_pool")
-        load_scales(cs_pool, c_scales, C_ROW0)
-        lm_col = load_by_query(lm[0, 0, :], "lm_col", nc.sync)
-        cw_pool = load_words(c_words, "cw_pool")
-        v_pool = [load_values(b) for b in range(BLOCKS)]
+        def load_values(b):
+            pool = relay.tile([P, TOKENS], F32, name=f"v_pool{b}", align_bytes=64, offset=b * POOL_BYTES)
+            nc.sync.dma_start(out=pool[:], in_=vT[b * P : (b + 1) * P, :])
+            return pool
 
-        ident = new("ident", [P, P], F32)
-        make_identity(nc, ident[:])
         one = new("one", [P, 1], F32)
         nc.gpsimd.memset(one[:], 1.0)
         eps = new("eps", [P, 1], F32)
-        nc.gpsimd.tensor_scalar(out=eps[:], in0=one[:], scalar1=EPS, scalar2=0.0, op0=ALU.mult, op1=ALU.add)
+        nc.scalar.activation(out=eps[:], in_=one[:], func=ACT.Copy, scale=EPS)
+
+        kw_pool = load_words(k_words, "kw_pool")
+        offsets = sbuf.tile([P, SLOTS // 16], U16, name="offsets")
+        nc.sync.dma_start(offsets[:], offs)
+        ks_pool = load_scales(k_scales, 0, "ks_pool")
+        q_raw = new("q_raw", [P, PACK, QUERIES], F32)
+        nc.sync.dma_start(out=q_raw[:], in_=qT[0].rearrange("(p j) q -> p j q", j=PACK))
+        cs_pool = load_scales(c_scales, C_ROW0, "cs_pool")
+        cw_pool = load_words(c_words, "cw_pool")
+        lm_col = load_columns(lm[0, 0, :], "lm_col", nc.sync)
+        us_col = load_columns(us[0, :, 0], "us_col", nc.sync)
+        v_pool = [load_values(b) for b in range(BLOCKS)]
+        ls_col = load_columns(ls[0, 0, :], "ls_col", nc.gpsimd)
+        l2_col = load_columns(l2[0, 0, :], "l2_col", nc.gpsimd)
+
+        ident = new("ident", [P, P], F32)
+        make_identity(nc, ident[:])
         neg_ls = negated(ls_col, "neg_ls")
         neg_l2 = negated(l2_col, "neg_l2")
         neg_lm = negated(lm_col, "neg_lm")
 
-        q_words = new("q_words", [P, QUERIES], U32)
-        q_scales = new("q_scales", [P, QUERIES], U8)
         squares = new("squares", [P, 2, TILES], F32)
         early = new("early", [P, SPLIT_TILES], F32)
+        q_words, q_scales = {}, {}
         first, second, taken, y_turned, y_bf, y_words, y_scales, sums = {}, {}, {}, {}, {}, {}, {}, {}
         v_picked, v_turned, v_bf, v_words, v_scales = {}, {}, {}, {}, {}
 
@@ -133,25 +127,29 @@ def tile_attend_at_diff_topk_kernel(tc, qT, k_words, k_scales, c_words, c_scales
             nc.vector.tensor_copy(out=picked[:], in_=pool[:].bitcast(dtype).indirect(offsets[:]))
             return picked
 
+        def round_queries():
+            q_bf = new("q_bf", [P, TILES, P, PACK], BF16)
+            dst = q_bf[:].rearrange("p i m j -> p m j i")
+            src = q_raw[:].rearrange("p j (m i) -> p m j i", i=TILES)
+            nc.vector.tensor_copy(out=dst[:, :VECTOR_ROWS], in_=src[:, :VECTOR_ROWS])
+            nc.scalar.activation(out=dst[:, VECTOR_ROWS:], in_=src[:, VECTOR_ROWS:], func=ACT.Copy)
+            return q_bf
+
         def quantise_queries(h):
-            q_bf = new(f"q_bf{h}", [P, 2, P, PACK], BF16)
-            nc.scalar.activation(
-                out=q_bf[:].rearrange("p r m j -> p m j r"),
-                in_=q_raw[h][:].rearrange("p j (m r) -> p m j r", r=2),
-                func=ACT.Copy,
-            )
-            cols = slice(h * HALF, (h + 1) * HALF)
+            q_words[h] = new(f"q_words{h}", [P, HALF], U32)
+            q_scales[h] = new(f"q_scales{h}", [P, HALF], U8)
             nc.vector.quantize_mx(
-                out=q_words[:, cols].bitcast(FP8X4), scales=q_scales[:, cols], in_=q_bf[:].rearrange("p r m j -> p (r m j)")
+                out=q_words[h][:].bitcast(FP8X4),
+                scales=q_scales[h][:],
+                in_=q_bf[:, 2 * h : 2 * h + 2].rearrange("p r m j -> p (r m j)"),
             )
 
-        def exp_scores(i, words, scales, neg_lse, name):
-            cols = slice(i * P, (i + 1) * P)
-            score = bank(i, [P, SLOTS])
+        def exp_scores(i, score, words, scales, neg_lse, name):
+            cols = slice((i % 2) * P, (i % 2 + 1) * P)
             nc.tensor.matmul_mx(
                 out=score[:],
-                lhsT=q_words[:, cols].bitcast(FP8X4),
-                lhsT_scale=q_scales[:, cols],
+                lhsT=q_words[i // 2][:, cols].bitcast(FP8X4),
+                lhsT_scale=q_scales[i // 2][:, cols],
                 rhs=words[:].bitcast(FP8X4),
                 rhs_scale=scales,
                 start=True,
@@ -167,24 +165,22 @@ def tile_attend_at_diff_topk_kernel(tc, qT, k_words, k_scales, c_words, c_scales
             return weights
 
         def first_weights(i):
-            first[i] = exp_scores(i, kw, ks[:], neg_ls, f"first{i}")
+            first[i] = exp_scores(i, bank(A_BANK[i], [P, SLOTS]), kw, ks[:], neg_ls, f"first{i}")
+
+        def turn_first(i):
+            y_turned[i] = bank(Y_BANK[i], [P, PACK, P])
+            for t in range(PACK):
+                nc.tensor.matmul(y_turned[i][:, t, :], first[i][:, t, :], ident[:], start=t == 0, stop=False, is_transpose=True)
 
         def second_weights(i):
-            second[i] = exp_scores(i, cw, cs[C_ROW0:P, :], neg_l2, f"second{i}")
+            score = bank(Z_BANK[i], [P, SLOTS])
+            second[i] = exp_scores(i, score, cw, cs[C_ROW0:P, :], neg_l2, f"second{i}")
 
         def take(i):
             taken[i] = new(f"taken{i}", [P, PACK, P], F32)
             nc.scalar.activation(out=taken[i][:], in_=second[i][:], func=ACT.Copy, scale=neg_lm[:, i : i + 1])
-
-        def turn_weights(i):
-            y_turned[i] = bank(i, [P, PACK, P])
-            if i == 0:
-                passes = [(first[i], t, t == 0, False) for t in range(PACK)]
-                passes += [(taken[i], t, False, t == PACK - 1) for t in range(PACK)]
-            else:
-                passes = [(src, t, src is first[i], src is taken[i]) for t in range(PACK) for src in (first[i], taken[i])]
-            for src, t, start, stop in passes:
-                nc.tensor.matmul(y_turned[i][:, t, :], src[:, t, :], ident[:], start=start, stop=stop, is_transpose=True)
+            for t in range(PACK):
+                nc.tensor.matmul(y_turned[i][:, t, :], taken[i][:, t, :], ident[:], start=False, stop=t == PACK - 1, is_transpose=True)
 
         def round_weights(i):
             y_bf[i] = new(f"y_bf{i}", [P, P, PACK], BF16)
@@ -203,36 +199,42 @@ def tile_attend_at_diff_topk_kernel(tc, qT, k_words, k_scales, c_words, c_scales
             )
 
         def gather_values(b):
-            v_picked[b] = new(f"v_picked{b}", [P, 2, P, 2], BF16)
-            nc.vector.tensor_copy(out=v_picked[b][:].rearrange("p u s r -> p s u r"), in_=v_pool[b][:].indirect(offsets[:]))
-
-        def turn_values(b):
-            pairs = v_picked[b][:].rearrange("p u s r -> p u (s r)").bitcast(F32)
+            v_picked[b] = new(f"v_picked{b}", [P, SLOTS], BF16)
+            nc.vector.tensor_copy(out=v_picked[b][:], in_=v_pool[b][:].indirect(offsets[:]))
+            pairs = v_picked[b][:].bitcast(F32)
             v_turned[b] = value_banks.tile([P, 2, P], F32, name="v_turned")
             for u in range(2):
-                nc.tensor.transpose(v_turned[b][:, u, :], pairs[:, u, :], ident[:])
+                nc.tensor.transpose(v_turned[b][:, u, :], pairs[:, u : SLOTS // 2 : 2], ident[:])
 
-        def copy_values(h):
-            v_bf[h] = new(f"v_bf{h}", [P, 2, P, PACK], BF16)
-            for k in range(2):
-                nc.scalar.copy(out=v_bf[h][:, k].bitcast(F32), in_=v_turned[2 * h + k][:].rearrange("p u e -> p e u"))
+        def copy_values(b):
+            v_bf[b] = new(f"v_bf{b}", [P, P, PACK], BF16) if b >= 2 else v_pair[:, b]
+            nc.scalar.copy(out=v_bf[b][:].bitcast(F32), in_=v_turned[b][:].rearrange("p u e -> p e u"))
 
-        def quantise_values(h):
-            v_words[h] = new(f"v_words{h}", [P, HALF], U32)
-            v_scales[h] = new(f"v_scales{h}", [P, HALF], U8)
+        def quantise_first_values():
+            v_words[0] = new("v_words0", [P, HALF], U32)
+            v_scales[0] = new("v_scales0", [P, HALF], U8)
             nc.vector.quantize_mx(
-                out=v_words[h][:].bitcast(FP8X4), scales=v_scales[h][:], in_=v_bf[h][:].rearrange("p k e t -> p (k e t)")
+                out=v_words[0][:].bitcast(FP8X4), scales=v_scales[0][:], in_=v_pair[:].rearrange("p k e t -> p (k e t)")
+            )
+
+        def quantise_last_values(b):
+            if b == 2:
+                v_words[1] = new("v_words1", [P, HALF], U32)
+                v_scales[1] = new("v_scales1", [P, HALF], U8)
+            cols = slice((b - 2) * P, (b - 1) * P)
+            nc.vector.quantize_mx(
+                out=v_words[1][:, cols].bitcast(FP8X4), scales=v_scales[1][:, cols], in_=v_bf[b][:].rearrange("p e t -> p (e t)")
             )
 
         def load_rsqrt_table():
             warm = new("warm", [P, 1], F32)
             nc.scalar.activation(
-                out=warm[:], in_=v_bf[0][:, 1, 0, 0:1], func=ACT.Abs_reciprocal_sqrt, scale=taken[TILES - 1][:, 0, 0:1], bias=one[:]
+                out=warm[:], in_=v_pair[:, 1, 0, 0:1], func=ACT.Abs_reciprocal_sqrt, scale=taken[TILES - 1][:, 0, 0:1], bias=one[:]
             )
 
         def product(i, halves):
             if halves[0] == 0:
-                sums[i] = bank(i, [P, DV])
+                sums[i] = bank(Y_BANK[i], [P, DV])
             for h in halves:
                 nc.tensor.matmul_mx(
                     out=sums[i][:, h * HALF : (h + 1) * HALF],
@@ -251,51 +253,53 @@ def tile_attend_at_diff_topk_kernel(tc, qT, k_words, k_scales, c_words, c_scales
                 accum_out=squares[:, halves[-1], i : i + 1],
             )
 
-        ks = gather_packed(ks_pool, U8, "ks")
-        quantise_queries(0)
+        v_pair = new("v_pair", [P, 2, P, PACK], BF16)
         kw = gather_packed(kw_pool, U32, "kw")
-        first_weights(0)
-        first_weights(1)
+        ks = gather_packed(ks_pool, U8, "ks")
+        q_bf = round_queries()
+        quantise_queries(0)
+        quantise_queries(1)
         cs = gather_packed(cs_pool, U8, "cs")
         cw = gather_packed(cw_pool, U32, "cw")
-        quantise_queries(1)
-        first_weights(2)
-        first_weights(3)
-
-        for step in (second_weights, take, turn_weights, gather_values):
-            step(0)
-            step(1)
-        for step in (second_weights, take):
-            step(2)
-            step(3)
-        turn_values(0)
-        turn_values(1)
+        for i in range(TILES):
+            first_weights(i)
+        for i in range(2):
+            second_weights(i)
+        for i in range(2):
+            turn_first(i)
+        gather_values(0)
+        gather_values(1)
+        take(0)
+        second_weights(2)
+        turn_first(2)
+        take(1)
+        second_weights(3)
+        turn_first(3)
+        take(2)
+        take(3)
         copy_values(0)
+        copy_values(1)
         load_rsqrt_table()
         round_weights(0)
-        quantise_weights(0)
-        turn_weights(2)
-        turn_weights(3)
-        gather_values(2)
-        turn_values(2)
         round_weights(1)
-        gather_values(3)
-        turn_values(3)
-        quantise_values(0)
+        quantise_weights(0)
+        gather_values(2)
+        copy_values(2)
         quantise_weights(1)
-        copy_values(1)
+        quantise_first_values()
+        gather_values(3)
+        copy_values(3)
         for i in range(SPLIT_TILES):
             product(i, [0])
-        nc.gpsimd.tensor_scalar(
-            out=early[:], in0=squares[:, 0, :SPLIT_TILES], scalar1=1.0 / DV, scalar2=EPS, op0=ALU.mult, op1=ALU.add
-        )
+        nc.scalar.activation(out=early[:], in_=squares[:, 0, :SPLIT_TILES], func=ACT.Identity, scale=1.0 / DV, bias=eps[:])
+        quantise_last_values(2)
         round_weights(2)
-        quantise_values(1)
+        quantise_last_values(3)
         quantise_weights(2)
         round_weights(3)
         quantise_weights(3)
 
-        rows_out = out[0].rearrange("(h m r) e -> m h r e", h=2, r=2)
+        rows_out = out[0].rearrange("(m i) e -> m i e", i=TILES)
         for i in range(TILES):
             split = i < SPLIT_TILES
             product(i, [1] if split else [0, 1])
@@ -312,4 +316,4 @@ def tile_attend_at_diff_topk_kernel(tc, qT, k_words, k_scales, c_words, c_scales
                 nc.vector.tensor_scalar(out=result[:], in0=sums[i][:], scalar1=rstd[:], scalar2=None, op0=ALU.mult)
             else:
                 nc.scalar.activation(out=result[:], in_=sums[i][:], func=ACT.Copy, scale=rstd[:])
-            nc.sync.dma_start(out=rows_out[:, i // 2, i % 2, :], in_=result[:])
+            nc.sync.dma_start(out=rows_out[:, i, :], in_=result[:])

@@ -34,15 +34,17 @@ Y_BANK = (0, 1, 4, 5)
 SPLIT_TILES = 2
 POOL_BYTES = TOKENS * 4
 
-AFTER_GATHER = {
-    "y_bf0": (1, 0),
-    "y_bf1": (1, 1024),
-    "y_words1": (2, 0),
-    "v_words0": (2, 2048),
-    "y_bf2": (3, 0),
-    "v_words1": (3, 2048),
-    "v_bf3": (3, 4096),
-    "y_bf3": (3, 4096),
+HOSTS = ("v_pool1", "v_pool2", "v_pool3", "v_bf3")
+TENANTS = {
+    "y_bf0": ("v_pool1", 0),
+    "y_bf1": ("v_pool2", 0),
+    "y_words0": ("v_pool2", 1024),
+    "v_words0": ("v_pool3", 0),
+    "v_words1": ("v_pool3", 1024),
+    "y_words1": ("v_pool3", 2048),
+    "y_bf2": ("v_pool3", 3072),
+    "y_words2": ("v_bf3", 0),
+    "y_bf3": ("v_bf3", 512),
 }
 
 
@@ -55,18 +57,16 @@ def tile_attend_at_diff_topk_kernel(tc, qT, k_words, k_scales, c_words, c_scales
         value_banks = ctx.enter_context(tc.psum_pool(name="value_banks", bufs=2))
 
         def new(name, shape, dtype):
-            if name in AFTER_GATHER:
-                block, start = AFTER_GATHER[name]
-                return relay.tile(shape, dtype, name=name, align_bytes=64, offset=block * POOL_BYTES + start)
+            host, start = TENANTS.get(name, (name, 0))
+            if host in HOSTS:
+                return relay.tile(shape, dtype, name=name, align_bytes=64, offset=HOSTS.index(host) * POOL_BYTES + start)
             return sbuf.tile(shape, dtype, name=name, align_bytes=64)
 
         def bank(i, shape):
             return tile_banks.tile(shape, F32, name="bank", tag=f"bank{i}")
 
-        def load_words(words, name):
-            pool = new(name, [P, TOKENS], I32)
+        def load_words(pool, words):
             nc.sync.dma_start(out=pool[:], in_=words[0].rearrange("p t r -> p (t r)").bitcast(I32))
-            return pool
 
         def load_scales(scales, row0, name):
             pool = new(name, [P, TOKENS // 4], I32)
@@ -87,7 +87,7 @@ def tile_attend_at_diff_topk_kernel(tc, qT, k_words, k_scales, c_words, c_scales
             return neg
 
         def load_values(b):
-            pool = relay.tile([P, TOKENS], F32, name=f"v_pool{b}", align_bytes=64, offset=b * POOL_BYTES)
+            pool = new(f"v_pool{b}", [P, TOKENS], F32)
             nc.sync.dma_start(out=pool[:], in_=vT[b * P : (b + 1) * P, :])
             return pool
 
@@ -96,14 +96,16 @@ def tile_attend_at_diff_topk_kernel(tc, qT, k_words, k_scales, c_words, c_scales
         eps = new("eps", [P, 1], F32)
         nc.scalar.activation(out=eps[:], in_=one[:], func=ACT.Copy, scale=EPS)
 
-        kw_pool = load_words(k_words, "kw_pool")
+        kw_pool = new("kw_pool", [P, TOKENS], I32)
+        load_words(kw_pool, k_words)
         offsets = sbuf.tile([P, SLOTS // 16], U16, name="offsets")
         nc.sync.dma_start(offsets[:], offs)
         ks_pool = load_scales(k_scales, 0, "ks_pool")
         q_raw = new("q_raw", [P, PACK, QUERIES], F32)
         nc.sync.dma_start(out=q_raw[:], in_=qT[0].rearrange("(p j) q -> p j q", j=PACK))
         cs_pool = load_scales(c_scales, C_ROW0, "cs_pool")
-        cw_pool = load_words(c_words, "cw_pool")
+        cw_pool = new("cw_pool", [P, TOKENS], I32)
+        load_words(cw_pool, c_words)
         lm_col = load_columns(lm[0, 0, :], "lm_col", nc.sync)
         us_col = load_columns(us[0, :, 0], "us_col", nc.sync)
         v_pool = [load_values(b) for b in range(BLOCKS)]
@@ -281,14 +283,14 @@ def tile_attend_at_diff_topk_kernel(tc, qT, k_words, k_scales, c_words, c_scales
         copy_values(1)
         load_rsqrt_table()
         round_weights(0)
-        round_weights(1)
-        quantise_weights(0)
         gather_values(2)
         copy_values(2)
-        quantise_weights(1)
-        quantise_first_values()
+        round_weights(1)
+        quantise_weights(0)
         gather_values(3)
         copy_values(3)
+        quantise_first_values()
+        quantise_weights(1)
         for i in range(SPLIT_TILES):
             product(i, [0])
         nc.scalar.activation(out=early[:], in_=squares[:, 0, :SPLIT_TILES], func=ACT.Identity, scale=1.0 / DV, bias=eps[:])

@@ -30,7 +30,7 @@ FLOPS = 3 * 2 * 512 * SLOTS * QUERIES
 VECTOR_ROWS = 84
 A_BANK = (0, 1, 2, 3)
 Z_BANK = (4, 5, 2, 3)
-Y_BANK = (0, 1, 4, 5)
+Y_BANK = (0, 1, 2, 3)
 SPLIT_TILES = 2
 POOL_BYTES = TOKENS * 4
 
@@ -169,10 +169,15 @@ def tile_attend_at_diff_topk_kernel(tc, qT, k_words, k_scales, c_words, c_scales
         def first_weights(i):
             first[i] = exp_scores(i, bank(A_BANK[i], [P, SLOTS]), kw, ks[:], neg_ls, f"first{i}")
 
-        def turn_first(i):
-            y_turned[i] = bank(Y_BANK[i], [P, PACK, P])
+        def turn(i, part, opens, closes):
+            if opens:
+                y_turned[i] = bank(Y_BANK[i], [P, PACK, P])
             for t in range(PACK):
-                nc.tensor.matmul(y_turned[i][:, t, :], first[i][:, t, :], ident[:], start=t == 0, stop=False, is_transpose=True)
+                start, stop = opens and t == 0, closes and t == PACK - 1
+                nc.tensor.matmul(y_turned[i][:, t, :], part[:, t, :], ident[:], start=start, stop=stop, is_transpose=True)
+
+        def turn_first(i):
+            turn(i, first[i], True, False)
 
         def second_weights(i):
             score = bank(Z_BANK[i], [P, SLOTS])
@@ -181,8 +186,7 @@ def tile_attend_at_diff_topk_kernel(tc, qT, k_words, k_scales, c_words, c_scales
         def take(i):
             taken[i] = new(f"taken{i}", [P, PACK, P], F32)
             nc.scalar.activation(out=taken[i][:], in_=second[i][:], func=ACT.Copy, scale=neg_lm[:, i : i + 1])
-            for t in range(PACK):
-                nc.tensor.matmul(y_turned[i][:, t, :], taken[i][:, t, :], ident[:], start=False, stop=t == PACK - 1, is_transpose=True)
+            turn(i, taken[i], False, True)
 
         def round_weights(i):
             y_bf[i] = new(f"y_bf{i}", [P, P, PACK], BF16)
@@ -231,7 +235,7 @@ def tile_attend_at_diff_topk_kernel(tc, qT, k_words, k_scales, c_words, c_scales
         def load_rsqrt_table():
             warm = new("warm", [P, 1], F32)
             nc.scalar.activation(
-                out=warm[:], in_=v_pair[:, 1, 0, 0:1], func=ACT.Abs_reciprocal_sqrt, scale=taken[TILES - 1][:, 0, 0:1], bias=one[:]
+                out=warm[:], in_=taken[TILES - 1][:, 0, 0:1], func=ACT.Abs_reciprocal_sqrt, bias=one[:]
             )
 
         def product(i, halves):
@@ -265,23 +269,21 @@ def tile_attend_at_diff_topk_kernel(tc, qT, k_words, k_scales, c_words, c_scales
         cw = gather_packed(cw_pool, U32, "cw")
         for i in range(TILES):
             first_weights(i)
-        for i in range(2):
-            second_weights(i)
-        for i in range(2):
-            turn_first(i)
+        second_weights(0)
+        second_weights(1)
+        turn_first(0)
+        turn_first(1)
         gather_values(0)
         gather_values(1)
-        take(0)
-        second_weights(2)
-        turn_first(2)
-        take(1)
-        second_weights(3)
-        turn_first(3)
-        take(2)
-        take(3)
+        for i in range(2):
+            take(i)
+            second_weights(i + 2)
+        for i in range(2, TILES):
+            turn_first(i)
+            take(i)
+        load_rsqrt_table()
         copy_values(0)
         copy_values(1)
-        load_rsqrt_table()
         round_weights(0)
         gather_values(2)
         copy_values(2)

@@ -30,7 +30,7 @@ FLOPS = 3 * 2 * 512 * SLOTS * QUERIES
 VECTOR_ROWS = 84
 A_BANK = (0, 1, 2, 3)
 Z_BANK = (4, 5, 2, 3)
-Y_BANK = (0, 1, 2, 3)
+Y_BANK = (0, 4, 2, 3)
 SPLIT_TILES = 2
 POOL_BYTES = TOKENS * 4
 

@@ -30,20 +30,16 @@ FLOPS = 3 * 2 * 512 * SLOTS * QUERIES
 VECTOR_ROWS = 84
 A_BANK = (0, 1, 2, 3)
 Z_BANK = (4, 5, 2, 3)
-Y_BANK = (0, 4, 2, 3)
-SPLIT_TILES = 2
+Y_BANK = (0, 1, 4, 5)
+V_BANK = (6, 7, 2, 3)
+SPLIT_TILES = 3
 POOL_BYTES = TOKENS * 4
 
-HOSTS = ("v_pool1", "v_pool2", "v_pool3", "v_bf3")
+HOSTS = ("v_pool3", "v_bf3", "v_picked1")
 TENANTS = {
-    "y_bf0": ("v_pool1", 0),
-    "y_bf1": ("v_pool2", 0),
-    "y_words0": ("v_pool2", 1024),
-    "v_words0": ("v_pool3", 0),
+    "taken3": ("v_picked1", 0),
     "v_words1": ("v_pool3", 1024),
-    "y_words1": ("v_pool3", 2048),
-    "y_bf2": ("v_pool3", 3072),
-    "y_words2": ("v_bf3", 0),
+    "y_bf2": ("v_pool3", 2048),
     "y_bf3": ("v_bf3", 512),
 }
 
@@ -54,7 +50,6 @@ def tile_attend_at_diff_topk_kernel(tc, qT, k_words, k_scales, c_words, c_scales
         sbuf = ctx.enter_context(tc.tile_pool(name="sbuf", bufs=1))
         relay = ctx.enter_context(tc.tile_pool(name="relay", bufs=1))
         tile_banks = ctx.enter_context(tc.psum_pool(name="tile_banks", bufs=1))
-        value_banks = ctx.enter_context(tc.psum_pool(name="value_banks", bufs=2))
 
         def new(name, shape, dtype):
             host, start = TENANTS.get(name, (name, 0))
@@ -106,9 +101,11 @@ def tile_attend_at_diff_topk_kernel(tc, qT, k_words, k_scales, c_words, c_scales
         cs_pool = load_scales(c_scales, C_ROW0, "cs_pool")
         cw_pool = new("cw_pool", [P, TOKENS], I32)
         load_words(cw_pool, c_words)
+        v_pool = [load_values(0)]
         lm_col = load_columns(lm[0, 0, :], "lm_col", nc.sync)
+        v_pool.append(load_values(1))
         us_col = load_columns(us[0, :, 0], "us_col", nc.sync)
-        v_pool = [load_values(b) for b in range(BLOCKS)]
+        v_pool.extend(load_values(b) for b in range(2, BLOCKS))
         ls_col = load_columns(ls[0, 0, :], "ls_col", nc.gpsimd)
         l2_col = load_columns(l2[0, 0, :], "l2_col", nc.gpsimd)
 
@@ -120,7 +117,7 @@ def tile_attend_at_diff_topk_kernel(tc, qT, k_words, k_scales, c_words, c_scales
 
         squares = new("squares", [P, 2, TILES], F32)
         early = new("early", [P, SPLIT_TILES], F32)
-        q_words, q_scales = {}, {}
+        q_words, q_scales, a_bank, z_bank = {}, {}, {}, {}
         first, second, taken, y_turned, y_bf, y_words, y_scales, sums = {}, {}, {}, {}, {}, {}, {}, {}
         v_picked, v_turned, v_bf, v_words, v_scales = {}, {}, {}, {}, {}
 
@@ -146,7 +143,7 @@ def tile_attend_at_diff_topk_kernel(tc, qT, k_words, k_scales, c_words, c_scales
                 in_=q_bf[:, 2 * h : 2 * h + 2].rearrange("p r m j -> p (r m j)"),
             )
 
-        def exp_scores(i, score, words, scales, neg_lse, name):
+        def scores(i, score, words, scales):
             cols = slice((i % 2) * P, (i % 2 + 1) * P)
             nc.tensor.matmul_mx(
                 out=score[:],
@@ -157,6 +154,9 @@ def tile_attend_at_diff_topk_kernel(tc, qT, k_words, k_scales, c_words, c_scales
                 start=True,
                 stop=True,
             )
+            return score
+
+        def exp_scores(i, score, neg_lse, name):
             weights = new(name, [P, PACK, P], F32)
             nc.scalar.activation(
                 out=weights[:],
@@ -166,8 +166,11 @@ def tile_attend_at_diff_topk_kernel(tc, qT, k_words, k_scales, c_words, c_scales
             )
             return weights
 
+        def first_scores(i):
+            a_bank[i] = scores(i, bank(A_BANK[i], [P, SLOTS]), kw, ks[:])
+
         def first_weights(i):
-            first[i] = exp_scores(i, bank(A_BANK[i], [P, SLOTS]), kw, ks[:], neg_ls, f"first{i}")
+            first[i] = exp_scores(i, a_bank[i], neg_ls, f"first{i}")
 
         def turn(i, part, opens, closes):
             if opens:
@@ -176,17 +179,20 @@ def tile_attend_at_diff_topk_kernel(tc, qT, k_words, k_scales, c_words, c_scales
                 start, stop = opens and t == 0, closes and t == PACK - 1
                 nc.tensor.matmul(y_turned[i][:, t, :], part[:, t, :], ident[:], start=start, stop=stop, is_transpose=True)
 
-        def turn_first(i):
-            turn(i, first[i], True, False)
+        def second_scores(i):
+            z_bank[i] = scores(i, bank(Z_BANK[i], [P, SLOTS]), cw, cs[C_ROW0:P, :])
 
         def second_weights(i):
-            score = bank(Z_BANK[i], [P, SLOTS])
-            second[i] = exp_scores(i, score, cw, cs[C_ROW0:P, :], neg_l2, f"second{i}")
+            second[i] = exp_scores(i, z_bank[i], neg_l2, f"second{i}")
 
         def take(i):
             taken[i] = new(f"taken{i}", [P, PACK, P], F32)
-            nc.scalar.activation(out=taken[i][:], in_=second[i][:], func=ACT.Copy, scale=neg_lm[:, i : i + 1])
-            turn(i, taken[i], False, True)
+            if i < 2:
+                nc.vector.tensor_scalar(
+                    out=taken[i][:], in0=second[i][:], scalar1=lm_col[:, i : i + 1], scalar2=-1.0, op0=ALU.mult, op1=ALU.mult
+                )
+            else:
+                nc.scalar.activation(out=taken[i][:], in_=second[i][:], func=ACT.Copy, scale=neg_lm[:, i : i + 1])
 
         def round_weights(i):
             y_bf[i] = new(f"y_bf{i}", [P, P, PACK], BF16)
@@ -208,7 +214,7 @@ def tile_attend_at_diff_topk_kernel(tc, qT, k_words, k_scales, c_words, c_scales
             v_picked[b] = new(f"v_picked{b}", [P, SLOTS], BF16)
             nc.vector.tensor_copy(out=v_picked[b][:], in_=v_pool[b][:].indirect(offsets[:]))
             pairs = v_picked[b][:].bitcast(F32)
-            v_turned[b] = value_banks.tile([P, 2, P], F32, name="v_turned")
+            v_turned[b] = bank(V_BANK[b], [P, 2, P])
             for u in range(2):
                 nc.tensor.transpose(v_turned[b][:, u, :], pairs[:, u : SLOTS // 2 : 2], ident[:])
 
@@ -259,6 +265,9 @@ def tile_attend_at_diff_topk_kernel(tc, qT, k_words, k_scales, c_words, c_scales
                 accum_out=squares[:, halves[-1], i : i + 1],
             )
 
+        def early_share(tiles):
+            nc.scalar.activation(out=early[:, tiles], in_=squares[:, 0, tiles], func=ACT.Identity, scale=1.0 / DV, bias=eps[:])
+
         v_pair = new("v_pair", [P, 2, P, PACK], BF16)
         kw = gather_packed(kw_pool, U32, "kw")
         ks = gather_packed(ks_pool, U8, "ks")
@@ -268,40 +277,43 @@ def tile_attend_at_diff_topk_kernel(tc, qT, k_words, k_scales, c_words, c_scales
         cs = gather_packed(cs_pool, U8, "cs")
         cw = gather_packed(cw_pool, U32, "cw")
         for i in range(TILES):
+            first_scores(i)
             first_weights(i)
-        second_weights(0)
-        second_weights(1)
-        turn_first(0)
-        turn_first(1)
+        for i in range(TILES):
+            second_scores(i)
+        for i in range(TILES):
+            second_weights(i)
+        for i in range(TILES):
+            turn(i, first[i], True, False)
         gather_values(0)
-        gather_values(1)
-        for i in range(2):
-            take(i)
-            second_weights(i + 2)
-        for i in range(2, TILES):
-            turn_first(i)
-            take(i)
-        load_rsqrt_table()
         copy_values(0)
+        for i in range(3):
+            take(i)
+            turn(i, taken[i], False, True)
+        gather_values(1)
         copy_values(1)
+        take(3)
+        turn(3, taken[3], False, True)
+        load_rsqrt_table()
         round_weights(0)
-        gather_values(2)
-        copy_values(2)
         round_weights(1)
         quantise_weights(0)
-        gather_values(3)
-        copy_values(3)
-        quantise_first_values()
         quantise_weights(1)
-        for i in range(SPLIT_TILES):
+        quantise_first_values()
+        for i in range(2):
             product(i, [0])
-        nc.scalar.activation(out=early[:], in_=squares[:, 0, :SPLIT_TILES], func=ACT.Identity, scale=1.0 / DV, bias=eps[:])
-        quantise_last_values(2)
+        early_share(slice(0, 2))
+        for b in range(2, BLOCKS):
+            gather_values(b)
+            copy_values(b)
         round_weights(2)
-        quantise_last_values(3)
+        quantise_last_values(2)
         quantise_weights(2)
+        quantise_last_values(3)
         round_weights(3)
         quantise_weights(3)
+        product(2, [0])
+        early_share(slice(2, 3))
 
         rows_out = out[0].rearrange("(m i) e -> m i e", i=TILES)
         for i in range(TILES):

@@ -23,24 +23,31 @@ TILES = QUERIES // P
 BLOCKS = DV // P
 HALF = 256
 SCALE_ROWS = 16
-C_ROW0 = 4
+LIST_ROWS = 16
+K_ROW0 = 4
 EPS = 1e-05
 FLOPS = 3 * 2 * 512 * SLOTS * QUERIES
 
-VECTOR_ROWS = 84
-A_BANK = (0, 1, 2, 3)
-Z_BANK = (4, 5, 2, 3)
-Y_BANK = (0, 1, 4, 5)
-V_BANK = (6, 7, 2, 3)
+VECTOR_ROWS = 52
+VECTOR_SLOTS = (512, 512, 0, 288)
 SPLIT_TILES = 3
 POOL_BYTES = TOKENS * 4
 
-HOSTS = ("v_pool3", "v_bf3", "v_picked1")
+HOSTS = ("kw_pool", "v_pool1", "v_pool3", "cs_pool")
 TENANTS = {
-    "taken3": ("v_picked1", 0),
-    "v_words1": ("v_pool3", 1024),
-    "y_bf2": ("v_pool3", 2048),
-    "y_bf3": ("v_bf3", 512),
+    "q_words": ("cs_pool", 0),
+    "taken0": ("kw_pool", 0),
+    "taken1": ("kw_pool", 2048),
+    "taken2": ("kw_pool", 4096),
+    "taken3": ("kw_pool", 6144),
+    "y_words0": ("v_pool1", 0),
+    "y_bf1": ("v_pool1", 1024),
+    "y_bf2": ("v_pool1", 2048),
+    "y_bf3": ("v_pool3", 0),
+    "v_bf2": ("v_pool3", 1024),
+    "squared0_0": ("v_pool3", 2048),
+    "squared1_0": ("v_pool3", 3072),
+    "squared2_0": ("v_pool3", 4096),
 }
 
 
@@ -49,7 +56,7 @@ def tile_attend_at_diff_topk_kernel(tc, qT, k_words, k_scales, c_words, c_scales
     with ExitStack() as ctx:
         sbuf = ctx.enter_context(tc.tile_pool(name="sbuf", bufs=1))
         relay = ctx.enter_context(tc.tile_pool(name="relay", bufs=1))
-        tile_banks = ctx.enter_context(tc.psum_pool(name="tile_banks", bufs=1))
+        banks = ctx.enter_context(tc.psum_pool(name="banks", bufs=1))
 
         def new(name, shape, dtype):
             host, start = TENANTS.get(name, (name, 0))
@@ -58,10 +65,12 @@ def tile_attend_at_diff_topk_kernel(tc, qT, k_words, k_scales, c_words, c_scales
             return sbuf.tile(shape, dtype, name=name, align_bytes=64)
 
         def bank(i, shape):
-            return tile_banks.tile(shape, F32, name="bank", tag=f"bank{i}")
+            return banks.tile(shape, F32, name="bank", tag=f"bank{i}")
 
-        def load_words(pool, words):
+        def load_words(words, name):
+            pool = new(name, [P, TOKENS], I32)
             nc.sync.dma_start(out=pool[:], in_=words[0].rearrange("p t r -> p (t r)").bitcast(I32))
+            return pool
 
         def load_scales(scales, row0, name):
             pool = new(name, [P, TOKENS // 4], I32)
@@ -91,35 +100,30 @@ def tile_attend_at_diff_topk_kernel(tc, qT, k_words, k_scales, c_words, c_scales
         eps = new("eps", [P, 1], F32)
         nc.scalar.activation(out=eps[:], in_=one[:], func=ACT.Copy, scale=EPS)
 
-        kw_pool = new("kw_pool", [P, TOKENS], I32)
-        load_words(kw_pool, k_words)
-        offsets = sbuf.tile([P, SLOTS // 16], U16, name="offsets")
-        nc.sync.dma_start(offsets[:], offs)
-        ks_pool = load_scales(k_scales, 0, "ks_pool")
         q_raw = new("q_raw", [P, PACK, QUERIES], F32)
         nc.sync.dma_start(out=q_raw[:], in_=qT[0].rearrange("(p j) q -> p j q", j=PACK))
-        cs_pool = load_scales(c_scales, C_ROW0, "cs_pool")
-        cw_pool = new("cw_pool", [P, TOKENS], I32)
-        load_words(cw_pool, c_words)
-        v_pool = [load_values(0)]
+        offsets = sbuf.tile([P, SLOTS // LIST_ROWS], U16, name="offsets")
+        nc.sync.dma_start(offsets[:], offs)
+        cs_pool = load_scales(c_scales, 0, "cs_pool")
+        cw_pool = load_words(c_words, "cw_pool")
+        ks_pool = load_scales(k_scales, K_ROW0, "ks_pool")
+        kw_pool = load_words(k_words, "kw_pool")
         lm_col = load_columns(lm[0, 0, :], "lm_col", nc.sync)
-        v_pool.append(load_values(1))
+        v_pool = [load_values(0)]
         us_col = load_columns(us[0, :, 0], "us_col", nc.sync)
-        v_pool.extend(load_values(b) for b in range(2, BLOCKS))
-        ls_col = load_columns(ls[0, 0, :], "ls_col", nc.gpsimd)
+        v_pool.extend(load_values(b) for b in range(1, BLOCKS))
         l2_col = load_columns(l2[0, 0, :], "l2_col", nc.gpsimd)
+        ls_col = load_columns(ls[0, 0, :], "ls_col", nc.gpsimd)
 
         ident = new("ident", [P, P], F32)
         make_identity(nc, ident[:])
-        neg_ls = negated(ls_col, "neg_ls")
         neg_l2 = negated(l2_col, "neg_l2")
-        neg_lm = negated(lm_col, "neg_lm")
+        neg_ls = negated(ls_col, "neg_ls")
 
         squares = new("squares", [P, 2, TILES], F32)
         early = new("early", [P, SPLIT_TILES], F32)
-        q_words, q_scales, a_bank, z_bank = {}, {}, {}, {}
         first, second, taken, y_turned, y_bf, y_words, y_scales, sums = {}, {}, {}, {}, {}, {}, {}, {}
-        v_picked, v_turned, v_bf, v_words, v_scales = {}, {}, {}, {}, {}
+        v_turned, v_bf, v_words, v_scales = {}, {}, {}, {}
 
         def gather_packed(pool, dtype, name):
             picked = new(name, [P, SLOTS], dtype)
@@ -127,28 +131,22 @@ def tile_attend_at_diff_topk_kernel(tc, qT, k_words, k_scales, c_words, c_scales
             return picked
 
         def round_queries():
-            q_bf = new("q_bf", [P, TILES, P, PACK], BF16)
-            dst = q_bf[:].rearrange("p i m j -> p m j i")
+            rounded = new("q_bf", [P, TILES, P, PACK], BF16)
+            dst = rounded[:].rearrange("p i m j -> p m j i")
             src = q_raw[:].rearrange("p j (m i) -> p m j i", i=TILES)
             nc.vector.tensor_copy(out=dst[:, :VECTOR_ROWS], in_=src[:, :VECTOR_ROWS])
             nc.scalar.activation(out=dst[:, VECTOR_ROWS:], in_=src[:, VECTOR_ROWS:], func=ACT.Copy)
-            return q_bf
+            return rounded
 
-        def quantise_queries(h):
-            q_words[h] = new(f"q_words{h}", [P, HALF], U32)
-            q_scales[h] = new(f"q_scales{h}", [P, HALF], U8)
-            nc.vector.quantize_mx(
-                out=q_words[h][:].bitcast(FP8X4),
-                scales=q_scales[h][:],
-                in_=q_bf[:, 2 * h : 2 * h + 2].rearrange("p r m j -> p (r m j)"),
-            )
+        def quantise(words, scales, rounded):
+            nc.vector.quantize_mx(out=words.bitcast(FP8X4), scales=scales, in_=rounded)
 
         def scores(i, score, words, scales):
-            cols = slice((i % 2) * P, (i % 2 + 1) * P)
+            cols = slice(i * P, (i + 1) * P)
             nc.tensor.matmul_mx(
                 out=score[:],
-                lhsT=q_words[i // 2][:, cols].bitcast(FP8X4),
-                lhsT_scale=q_scales[i // 2][:, cols],
+                lhsT=q_words[:, cols].bitcast(FP8X4),
+                lhsT_scale=q_scales[:, cols],
                 rhs=words[:].bitcast(FP8X4),
                 rhs_scale=scales,
                 start=True,
@@ -166,33 +164,19 @@ def tile_attend_at_diff_topk_kernel(tc, qT, k_words, k_scales, c_words, c_scales
             )
             return weights
 
-        def first_scores(i):
-            a_bank[i] = scores(i, bank(A_BANK[i], [P, SLOTS]), kw, ks[:])
-
-        def first_weights(i):
-            first[i] = exp_scores(i, a_bank[i], neg_ls, f"first{i}")
-
-        def turn(i, part, opens, closes):
-            if opens:
-                y_turned[i] = bank(Y_BANK[i], [P, PACK, P])
-            for t in range(PACK):
-                start, stop = opens and t == 0, closes and t == PACK - 1
-                nc.tensor.matmul(y_turned[i][:, t, :], part[:, t, :], ident[:], start=start, stop=stop, is_transpose=True)
-
-        def second_scores(i):
-            z_bank[i] = scores(i, bank(Z_BANK[i], [P, SLOTS]), cw, cs[C_ROW0:P, :])
-
-        def second_weights(i):
-            second[i] = exp_scores(i, z_bank[i], neg_l2, f"second{i}")
-
         def take(i):
             taken[i] = new(f"taken{i}", [P, PACK, P], F32)
-            if i < 2:
-                nc.vector.tensor_scalar(
-                    out=taken[i][:], in0=second[i][:], scalar1=lm_col[:, i : i + 1], scalar2=-1.0, op0=ALU.mult, op1=ALU.mult
+            nc.vector.tensor_scalar(
+                out=taken[i][:], in0=second[i][:], scalar1=lm_col[:, i : i + 1], scalar2=-1.0, op0=ALU.mult, op1=ALU.mult
+            )
+
+        def turn_weights(i):
+            y_turned[i] = bank(i, [P, PACK, P])
+            parts = [(part, t) for part in (taken[i], first[i]) for t in range(PACK)]
+            for n, (part, t) in enumerate(parts):
+                nc.tensor.matmul(
+                    y_turned[i][:, t, :], part[:, t, :], ident[:], start=n == 0, stop=n == len(parts) - 1, is_transpose=True
                 )
-            else:
-                nc.scalar.activation(out=taken[i][:], in_=second[i][:], func=ACT.Copy, scale=neg_lm[:, i : i + 1])
 
         def round_weights(i):
             y_bf[i] = new(f"y_bf{i}", [P, P, PACK], BF16)
@@ -206,15 +190,17 @@ def tile_attend_at_diff_topk_kernel(tc, qT, k_words, k_scales, c_words, c_scales
         def quantise_weights(i):
             y_words[i] = new(f"y_words{i}", [P, P], U32)
             y_scales[i] = new(f"y_scales{i}", [P, P], U8)
-            nc.vector.quantize_mx(
-                out=y_words[i][:].bitcast(FP8X4), scales=y_scales[i][:], in_=y_bf[i][:].rearrange("p m t -> p (m t)")
-            )
+            quantise(y_words[i][:], y_scales[i][:], y_bf[i][:].rearrange("p m t -> p (m t)"))
 
         def gather_values(b):
-            v_picked[b] = new(f"v_picked{b}", [P, SLOTS], BF16)
-            nc.vector.tensor_copy(out=v_picked[b][:], in_=v_pool[b][:].indirect(offsets[:]))
-            pairs = v_picked[b][:].bitcast(F32)
-            v_turned[b] = bank(V_BANK[b], [P, 2, P])
+            picked = new(f"v_picked{b}", [P, SLOTS], BF16)
+            cut = VECTOR_SLOTS[b]
+            if cut > 0:
+                nc.vector.tensor_copy(out=picked[:, :cut], in_=v_pool[b][:].indirect(offsets[:, : cut // LIST_ROWS]))
+            if cut < SLOTS:
+                nc.scalar.activation(out=picked[:, cut:], in_=v_pool[b][:].indirect(offsets[:, cut // LIST_ROWS :]), func=ACT.Copy)
+            pairs = picked[:].bitcast(F32)
+            v_turned[b] = bank(2 * TILES - 1 - b, [P, 2, P])
             for u in range(2):
                 nc.tensor.transpose(v_turned[b][:, u, :], pairs[:, u : SLOTS // 2 : 2], ident[:])
 
@@ -222,41 +208,32 @@ def tile_attend_at_diff_topk_kernel(tc, qT, k_words, k_scales, c_words, c_scales
             v_bf[b] = new(f"v_bf{b}", [P, P, PACK], BF16) if b >= 2 else v_pair[:, b]
             nc.scalar.copy(out=v_bf[b][:].bitcast(F32), in_=v_turned[b][:].rearrange("p u e -> p e u"))
 
-        def quantise_first_values():
-            v_words[0] = new("v_words0", [P, HALF], U32)
-            v_scales[0] = new("v_scales0", [P, HALF], U8)
-            nc.vector.quantize_mx(
-                out=v_words[0][:].bitcast(FP8X4), scales=v_scales[0][:], in_=v_pair[:].rearrange("p k e t -> p (k e t)")
-            )
-
-        def quantise_last_values(b):
-            if b == 2:
-                v_words[1] = new("v_words1", [P, HALF], U32)
-                v_scales[1] = new("v_scales1", [P, HALF], U8)
-            cols = slice((b - 2) * P, (b - 1) * P)
-            nc.vector.quantize_mx(
-                out=v_words[1][:, cols].bitcast(FP8X4), scales=v_scales[1][:, cols], in_=v_bf[b][:].rearrange("p e t -> p (e t)")
-            )
+        def quantise_values(blocks, rounded):
+            h = blocks[0] // 2
+            if blocks[0] % 2 == 0:
+                v_words[h] = new(f"v_words{h}", [P, HALF], U32)
+                v_scales[h] = new(f"v_scales{h}", [P, HALF], U8)
+            cols = slice(blocks[0] % 2 * P, (blocks[-1] % 2 + 1) * P)
+            quantise(v_words[h][:, cols], v_scales[h][:, cols], rounded)
 
         def load_rsqrt_table():
             warm = new("warm", [P, 1], F32)
-            nc.scalar.activation(
-                out=warm[:], in_=taken[TILES - 1][:, 0, 0:1], func=ACT.Abs_reciprocal_sqrt, bias=one[:]
+            nc.scalar.activation(out=warm[:], in_=first[TILES - 1][:, 0, 0:1], func=ACT.Abs_reciprocal_sqrt, bias=one[:])
+
+        def product(i, h):
+            if h == 0:
+                sums[i] = bank(i, [P, DV])
+            nc.tensor.matmul_mx(
+                out=sums[i][:, h * HALF : (h + 1) * HALF],
+                lhsT=y_words[i][:].bitcast(FP8X4),
+                lhsT_scale=y_scales[i][:],
+                rhs=v_words[h][:].bitcast(FP8X4),
+                rhs_scale=v_scales[h][:],
+                start=True,
+                stop=True,
             )
 
-        def product(i, halves):
-            if halves[0] == 0:
-                sums[i] = bank(Y_BANK[i], [P, DV])
-            for h in halves:
-                nc.tensor.matmul_mx(
-                    out=sums[i][:, h * HALF : (h + 1) * HALF],
-                    lhsT=y_words[i][:].bitcast(FP8X4),
-                    lhsT_scale=y_scales[i][:],
-                    rhs=v_words[h][:].bitcast(FP8X4),
-                    rhs_scale=v_scales[h][:],
-                    start=True,
-                    stop=True,
-                )
+        def sum_squares(i, halves):
             squared = new(f"squared{i}_{halves[-1]}", [P, len(halves) * HALF], BF16)
             nc.scalar.activation(
                 out=squared[:],
@@ -265,60 +242,59 @@ def tile_attend_at_diff_topk_kernel(tc, qT, k_words, k_scales, c_words, c_scales
                 accum_out=squares[:, halves[-1], i : i + 1],
             )
 
-        def early_share(tiles):
-            nc.scalar.activation(out=early[:, tiles], in_=squares[:, 0, tiles], func=ACT.Identity, scale=1.0 / DV, bias=eps[:])
-
-        v_pair = new("v_pair", [P, 2, P, PACK], BF16)
-        kw = gather_packed(kw_pool, U32, "kw")
-        ks = gather_packed(ks_pool, U8, "ks")
         q_bf = round_queries()
-        quantise_queries(0)
-        quantise_queries(1)
         cs = gather_packed(cs_pool, U8, "cs")
+        q_words = new("q_words", [P, QUERIES], U32)
+        q_scales = new("q_scales", [P, QUERIES], U8)
+        quantise(q_words[:], q_scales[:], q_bf[:].rearrange("p i m j -> p (i m j)"))
         cw = gather_packed(cw_pool, U32, "cw")
+        ks = gather_packed(ks_pool, U8, "ks")
+        kw = gather_packed(kw_pool, U32, "kw")
         for i in range(TILES):
-            first_scores(i)
-            first_weights(i)
+            second[i] = exp_scores(i, scores(i, bank(i, [P, SLOTS]), cw, cs[:]), neg_l2, f"second{i}")
         for i in range(TILES):
-            second_scores(i)
+            first[i] = exp_scores(i, scores(i, bank(TILES + i, [P, SLOTS]), kw, ks[K_ROW0:P, :]), neg_ls, f"first{i}")
+        load_rsqrt_table()
         for i in range(TILES):
-            second_weights(i)
-        for i in range(TILES):
-            turn(i, first[i], True, False)
+            take(i)
+        v_pair = new("v_pair", [P, 2, P, PACK], BF16)
+        turn_weights(0)
         gather_values(0)
         copy_values(0)
-        for i in range(3):
-            take(i)
-            turn(i, taken[i], False, True)
+        round_weights(0)
+        turn_weights(1)
         gather_values(1)
         copy_values(1)
-        take(3)
-        turn(3, taken[3], False, True)
-        load_rsqrt_table()
-        round_weights(0)
-        round_weights(1)
+        turn_weights(2)
+        turn_weights(3)
         quantise_weights(0)
-        quantise_weights(1)
-        quantise_first_values()
-        for i in range(2):
-            product(i, [0])
-        early_share(slice(0, 2))
-        for b in range(2, BLOCKS):
-            gather_values(b)
-            copy_values(b)
+        round_weights(1)
         round_weights(2)
-        quantise_last_values(2)
+        quantise_weights(1)
+        quantise_values([0, 1], v_pair[:].rearrange("p k e t -> p (k e t)"))
         quantise_weights(2)
-        quantise_last_values(3)
+        gather_values(2)
+        for i in range(SPLIT_TILES):
+            product(i, 0)
+        gather_values(3)
+        copy_values(2)
+        sum_squares(0, [0])
+        sum_squares(1, [0])
+        copy_values(3)
+        sum_squares(2, [0])
+        nc.scalar.activation(out=early[:], in_=squares[:, 0, :SPLIT_TILES], func=ACT.Identity, scale=1.0 / DV, bias=eps[:])
         round_weights(3)
+        quantise_values([2], v_bf[2][:].rearrange("p e t -> p (e t)"))
         quantise_weights(3)
-        product(2, [0])
-        early_share(slice(2, 3))
+        quantise_values([3], v_bf[3][:].rearrange("p e t -> p (e t)"))
 
         rows_out = out[0].rearrange("(m i) e -> m i e", i=TILES)
         for i in range(TILES):
             split = i < SPLIT_TILES
-            product(i, [1] if split else [0, 1])
+            halves = [1] if split else [0, 1]
+            for h in halves:
+                product(i, h)
+            sum_squares(i, halves)
             rstd = new(f"rstd{i}", [P, 1], F32)
             nc.scalar.activation(
                 out=rstd[:],
@@ -328,8 +304,5 @@ def tile_attend_at_diff_topk_kernel(tc, qT, k_words, k_scales, c_words, c_scales
                 bias=early[:, i : i + 1] if split else eps[:],
             )
             result = new(f"result{i}", [P, DV], F32)
-            if i < TILES - 1:
-                nc.vector.tensor_scalar(out=result[:], in0=sums[i][:], scalar1=rstd[:], scalar2=None, op0=ALU.mult)
-            else:
-                nc.scalar.activation(out=result[:], in_=sums[i][:], func=ACT.Copy, scale=rstd[:])
+            nc.vector.tensor_scalar(out=result[:], in0=sums[i][:], scalar1=rstd[:], scalar2=None, op0=ALU.mult)
             nc.sync.dma_start(out=rows_out[:, i, :], in_=result[:])

@@ -43,7 +43,8 @@ TENANTS = {
     "y_words0": ("v_pool1", 0),
     "y_bf1": ("v_pool1", 1024),
     "y_bf2": ("v_pool1", 2048),
-    "y_bf3": ("v_pool3", 0),
+    "y_bf3": ("v_pool1", 3072),
+    "y_words3": ("v_pool3", 0),
     "v_bf2": ("v_pool3", 1024),
     "squared0_0": ("v_pool3", 2048),
     "squared1_0": ("v_pool3", 3072),
@@ -206,7 +207,8 @@ def tile_attend_at_diff_topk_kernel(tc, qT, k_words, k_scales, c_words, c_scales
 
         def copy_values(b):
             v_bf[b] = new(f"v_bf{b}", [P, P, PACK], BF16) if b >= 2 else v_pair[:, b]
-            nc.scalar.copy(out=v_bf[b][:].bitcast(F32), in_=v_turned[b][:].rearrange("p u e -> p e u"))
+            copy = nc.vector.tensor_copy if b == 2 else nc.scalar.copy
+            copy(out=v_bf[b][:].bitcast(F32), in_=v_turned[b][:].rearrange("p u e -> p e u"))
 
         def quantise_values(blocks, rounded):
             h = blocks[0] // 2
@@ -272,20 +274,20 @@ def tile_attend_at_diff_topk_kernel(tc, qT, k_words, k_scales, c_words, c_scales
         round_weights(2)
         quantise_weights(1)
         quantise_values([0, 1], v_pair[:].rearrange("p k e t -> p (k e t)"))
+        round_weights(3)
         quantise_weights(2)
         gather_values(2)
-        for i in range(SPLIT_TILES):
+        for i in range(TILES - 1):
             product(i, 0)
         gather_values(3)
+        quantise_weights(3)
         copy_values(2)
         sum_squares(0, [0])
         sum_squares(1, [0])
         copy_values(3)
         sum_squares(2, [0])
         nc.scalar.activation(out=early[:], in_=squares[:, 0, :SPLIT_TILES], func=ACT.Identity, scale=1.0 / DV, bias=eps[:])
-        round_weights(3)
         quantise_values([2], v_bf[2][:].rearrange("p e t -> p (e t)"))
-        quantise_weights(3)
         quantise_values([3], v_bf[3][:].rearrange("p e t -> p (e t)"))
 
         rows_out = out[0].rearrange("(m i) e -> m i e", i=TILES)
@@ -304,5 +306,8 @@ def tile_attend_at_diff_topk_kernel(tc, qT, k_words, k_scales, c_words, c_scales
                 bias=early[:, i : i + 1] if split else eps[:],
             )
             result = new(f"result{i}", [P, DV], F32)
-            nc.vector.tensor_scalar(out=result[:], in0=sums[i][:], scalar1=rstd[:], scalar2=None, op0=ALU.mult)
+            if i < TILES - 1:
+                nc.vector.tensor_scalar(out=result[:], in0=sums[i][:], scalar1=rstd[:], scalar2=None, op0=ALU.mult)
+            else:
+                nc.scalar.activation(out=result[:], in_=sums[i][:], func=ACT.Copy, scale=rstd[:])
             nc.sync.dma_start(out=rows_out[:, i, :], in_=result[:])

@@ -29,7 +29,7 @@ EPS = 1e-05
 FLOPS = 3 * 2 * 512 * SLOTS * QUERIES
 
 VECTOR_ROWS = 52
-VECTOR_SLOTS = (512, 512, 0, 288)
+VECTOR_SLOTS = (512, 512, 0, 256)
 SPLIT_TILES = 3
 POOL_BYTES = TOKENS * 4
 
@@ -222,15 +222,15 @@ def tile_attend_at_diff_topk_kernel(tc, qT, k_words, k_scales, c_words, c_scales
             warm = new("warm", [P, 1], F32)
             nc.scalar.activation(out=warm[:], in_=first[TILES - 1][:, 0, 0:1], func=ACT.Abs_reciprocal_sqrt, bias=one[:])
 
-        def product(i, h):
+        def product(i, h, cols=slice(0, HALF)):
             if h == 0:
                 sums[i] = bank(i, [P, DV])
             nc.tensor.matmul_mx(
-                out=sums[i][:, h * HALF : (h + 1) * HALF],
+                out=sums[i][:, h * HALF + cols.start : h * HALF + cols.stop],
                 lhsT=y_words[i][:].bitcast(FP8X4),
                 lhsT_scale=y_scales[i][:],
-                rhs=v_words[h][:].bitcast(FP8X4),
-                rhs_scale=v_scales[h][:],
+                rhs=v_words[h][:, cols].bitcast(FP8X4),
+                rhs_scale=v_scales[h][:, cols],
                 start=True,
                 stop=True,
             )
@@ -288,6 +288,7 @@ def tile_attend_at_diff_topk_kernel(tc, qT, k_words, k_scales, c_words, c_scales
         sum_squares(2, [0])
         nc.scalar.activation(out=early[:], in_=squares[:, 0, :SPLIT_TILES], func=ACT.Identity, scale=1.0 / DV, bias=eps[:])
         quantise_values([2], v_bf[2][:].rearrange("p e t -> p (e t)"))
+        product(0, 1, slice(0, P))
         quantise_values([3], v_bf[3][:].rearrange("p e t -> p (e t)"))
 
         rows_out = out[0].rearrange("(m i) e -> m i e", i=TILES)
@@ -295,7 +296,7 @@ def tile_attend_at_diff_topk_kernel(tc, qT, k_words, k_scales, c_words, c_scales
             split = i < SPLIT_TILES
             halves = [1] if split else [0, 1]
             for h in halves:
-                product(i, h)
+                product(i, h, slice(P if i == 0 else 0, HALF))
             sum_squares(i, halves)
             rstd = new(f"rstd{i}", [P, 1], F32)
             nc.scalar.activation(

from contextlib import ExitStack

import concourse.mybir as mybir
from concourse.masks import make_identity

F32 = mybir.dt.float32
BF16 = mybir.dt.bfloat16
I32 = mybir.dt.int32
U32 = mybir.dt.uint32
U16 = mybir.dt.uint16
U8 = mybir.dt.uint8
FP8X4 = mybir.dt.float8_e4m3fn_x4
ACT = mybir.ActivationFunctionType
ALU = mybir.AluOpType

P = 128
PACK = 4
TOKENS = 2048
SLOTS = 512
QUERIES = 512
DV = 512
TILES = QUERIES // P
BLOCKS = DV // P
HALF = 256
SCALE_ROWS = 16
LIST_ROWS = 16
K_ROW0 = 4
EPS = 1e-05
FLOPS = 3 * 2 * 512 * SLOTS * QUERIES

VECTOR_ROWS = 52
VECTOR_SLOTS = (512, 512, 0, 256)
SPLIT_TILES = 3
POOL_BYTES = TOKENS * 4

HOSTS = ("kw_pool", "v_pool1", "v_pool3", "cs_pool")
TENANTS = {
    "q_words": ("cs_pool", 0),
    "taken0": ("kw_pool", 0),
    "taken1": ("kw_pool", 2048),
    "taken2": ("kw_pool", 4096),
    "taken3": ("kw_pool", 6144),
    "y_words0": ("v_pool1", 0),
    "y_bf1": ("v_pool1", 1024),
    "y_bf2": ("v_pool1", 2048),
    "y_bf3": ("v_pool1", 3072),
    "y_words3": ("v_pool3", 0),
    "v_bf2": ("v_pool3", 1024),
    "squared0_0": ("v_pool3", 2048),
    "squared1_0": ("v_pool3", 3072),
    "squared2_0": ("v_pool3", 4096),
}


def tile_attend_at_diff_topk_kernel(tc, qT, k_words, k_scales, c_words, c_scales, vT, ls, lm, l2, us, offs, out):
    nc = tc.nc
    with ExitStack() as ctx:
        sbuf = ctx.enter_context(tc.tile_pool(name="sbuf", bufs=1))
        relay = ctx.enter_context(tc.tile_pool(name="relay", bufs=1))
        banks = ctx.enter_context(tc.psum_pool(name="banks", bufs=1))

        def new(name, shape, dtype):
            host, start = TENANTS.get(name, (name, 0))
            if host in HOSTS:
                return relay.tile(shape, dtype, name=name, align_bytes=64, offset=HOSTS.index(host) * POOL_BYTES + start)
            return sbuf.tile(shape, dtype, name=name, align_bytes=64)

        def bank(i, shape):
            return banks.tile(shape, F32, name="bank", tag=f"bank{i}")

        def load_words(words, name):
            pool = new(name, [P, TOKENS], I32)
            nc.sync.dma_start(out=pool[:], in_=words[0].rearrange("p t r -> p (t r)").bitcast(I32))
            return pool

        def load_scales(scales, row0, name):
            pool = new(name, [P, TOKENS // 4], I32)
            nc.vector.memset(pool[:], 0)
            rows = scales[0].bitcast(I32)
            for r in range(4):
                nc.sync.dma_start(out=pool[row0 + r : P : 32, :], in_=rows[r:SCALE_ROWS:4, :])
            return pool

        def load_columns(vec, name, queue):
            col = new(name, [P, PACK], F32)
            queue.dma_start(out=col[:], in_=vec.rearrange("(p t) -> p t", t=PACK))
            return col

        def negated(col, name):
            neg = new(name, [P, TILES], F32)
            nc.gpsimd.tensor_scalar(out=neg[:], in0=col[:], scalar1=-1.0, scalar2=0.0, op0=ALU.mult, op1=ALU.add)
            return neg

        def load_values(b):
            pool = new(f"v_pool{b}", [P, TOKENS], F32)
            nc.sync.dma_start(out=pool[:], in_=vT[b * P : (b + 1) * P, :])
            return pool

        one = new("one", [P, 1], F32)
        nc.gpsimd.memset(one[:], 1.0)
        eps = new("eps", [P, 1], F32)
        nc.scalar.activation(out=eps[:], in_=one[:], func=ACT.Copy, scale=EPS)

        q_raw = new("q_raw", [P, PACK, QUERIES], F32)
        nc.sync.dma_start(out=q_raw[:], in_=qT[0].rearrange("(p j) q -> p j q", j=PACK))
        offsets = sbuf.tile([P, SLOTS // LIST_ROWS], U16, name="offsets")
        nc.sync.dma_start(offsets[:], offs)
        cs_pool = load_scales(c_scales, 0, "cs_pool")
        cw_pool = load_words(c_words, "cw_pool")
        ks_pool = load_scales(k_scales, K_ROW0, "ks_pool")
        kw_pool = load_words(k_words, "kw_pool")
        lm_col = load_columns(lm[0, 0, :], "lm_col", nc.sync)
        v_pool = [load_values(0)]
        us_col = load_columns(us[0, :, 0], "us_col", nc.sync)
        v_pool.extend(load_values(b) for b in range(1, BLOCKS))
        l2_col = load_columns(l2[0, 0, :], "l2_col", nc.gpsimd)
        ls_col = load_columns(ls[0, 0, :], "ls_col", nc.gpsimd)

        ident = new("ident", [P, P], F32)
        make_identity(nc, ident[:])
        neg_l2 = negated(l2_col, "neg_l2")
        neg_ls = negated(ls_col, "neg_ls")

        squares = new("squares", [P, 2, TILES], F32)
        early = new("early", [P, SPLIT_TILES], F32)
        first, second, taken, y_turned, y_bf, y_words, y_scales, sums = {}, {}, {}, {}, {}, {}, {}, {}
        v_turned, v_bf, v_words, v_scales = {}, {}, {}, {}

        def gather_packed(pool, dtype, name):
            picked = new(name, [P, SLOTS], dtype)
            nc.vector.tensor_copy(out=picked[:], in_=pool[:].bitcast(dtype).indirect(offsets[:]))
            return picked

        def round_queries():
            rounded = new("q_bf", [P, TILES, P, PACK], BF16)
            dst = rounded[:].rearrange("p i m j -> p m j i")
            src = q_raw[:].rearrange("p j (m i) -> p m j i", i=TILES)
            nc.vector.tensor_copy(out=dst[:, :VECTOR_ROWS], in_=src[:, :VECTOR_ROWS])
            nc.scalar.activation(out=dst[:, VECTOR_ROWS:], in_=src[:, VECTOR_ROWS:], func=ACT.Copy)
            return rounded

        def quantise(words, scales, rounded):
            nc.vector.quantize_mx(out=words.bitcast(FP8X4), scales=scales, in_=rounded)

        def scores(i, score, words, scales):
            cols = slice(i * P, (i + 1) * P)
            nc.tensor.matmul_mx(
                out=score[:],
                lhsT=q_words[:, cols].bitcast(FP8X4),
                lhsT_scale=q_scales[:, cols],
                rhs=words[:].bitcast(FP8X4),
                rhs_scale=scales,
                start=True,
                stop=True,
            )
            return score

        def exp_scores(i, score, neg_lse, name):
            weights = new(name, [P, PACK, P], F32)
            nc.scalar.activation(
                out=weights[:],
                in_=score[:].rearrange("p (s t) -> p t s", t=PACK),
                func=ACT.Exp,
                bias=neg_lse[:, i : i + 1],
            )
            return weights

        def take(i):
            taken[i] = new(f"taken{i}", [P, PACK, P], F32)
            nc.vector.tensor_scalar(
                out=taken[i][:], in0=second[i][:], scalar1=lm_col[:, i : i + 1], scalar2=-1.0, op0=ALU.mult, op1=ALU.mult
            )

        def turn_weights(i):
            y_turned[i] = bank(i, [P, PACK, P])
            parts = [(part, t) for part in (taken[i], first[i]) for t in range(PACK)]
            for n, (part, t) in enumerate(parts):
                nc.tensor.matmul(
                    y_turned[i][:, t, :], part[:, t, :], ident[:], start=n == 0, stop=n == len(parts) - 1, is_transpose=True
                )

        def round_weights(i):
            y_bf[i] = new(f"y_bf{i}", [P, P, PACK], BF16)
            nc.vector.tensor_tensor(
                out=y_bf[i][:],
                in0=y_turned[i][:].rearrange("p t m -> p m t"),
                in1=us_col[:].unsqueeze(1).to_broadcast([P, P, PACK]),
                op=ALU.mult,
            )

        def quantise_weights(i):
            y_words[i] = new(f"y_words{i}", [P, P], U32)
            y_scales[i] = new(f"y_scales{i}", [P, P], U8)
            quantise(y_words[i][:], y_scales[i][:], y_bf[i][:].rearrange("p m t -> p (m t)"))

        def gather_values(b):
            picked = new(f"v_picked{b}", [P, SLOTS], BF16)
            cut = VECTOR_SLOTS[b]
            if cut > 0:
                nc.vector.tensor_copy(out=picked[:, :cut], in_=v_pool[b][:].indirect(offsets[:, : cut // LIST_ROWS]))
            if cut < SLOTS:
                nc.scalar.activation(out=picked[:, cut:], in_=v_pool[b][:].indirect(offsets[:, cut // LIST_ROWS :]), func=ACT.Copy)
            pairs = picked[:].bitcast(F32)
            v_turned[b] = bank(2 * TILES - 1 - b, [P, 2, P])
            for u in range(2):
                nc.tensor.transpose(v_turned[b][:, u, :], pairs[:, u : SLOTS // 2 : 2], ident[:])

        def copy_values(b):
            v_bf[b] = new(f"v_bf{b}", [P, P, PACK], BF16) if b >= 2 else v_pair[:, b]
            copy = nc.vector.tensor_copy if b == 2 else nc.scalar.copy
            copy(out=v_bf[b][:].bitcast(F32), in_=v_turned[b][:].rearrange("p u e -> p e u"))

        def quantise_values(blocks, rounded):
            h = blocks[0] // 2
            if blocks[0] % 2 == 0:
                v_words[h] = new(f"v_words{h}", [P, HALF], U32)
                v_scales[h] = new(f"v_scales{h}", [P, HALF], U8)
            cols = slice(blocks[0] % 2 * P, (blocks[-1] % 2 + 1) * P)
            quantise(v_words[h][:, cols], v_scales[h][:, cols], rounded)

        def load_rsqrt_table():
            warm = new("warm", [P, 1], F32)
            nc.scalar.activation(out=warm[:], in_=first[TILES - 1][:, 0, 0:1], func=ACT.Abs_reciprocal_sqrt, bias=one[:])

        def product(i, h, cols=slice(0, HALF)):
            if h == 0:
                sums[i] = bank(i, [P, DV])
            nc.tensor.matmul_mx(
                out=sums[i][:, h * HALF + cols.start : h * HALF + cols.stop],
                lhsT=y_words[i][:].bitcast(FP8X4),
                lhsT_scale=y_scales[i][:],
                rhs=v_words[h][:, cols].bitcast(FP8X4),
                rhs_scale=v_scales[h][:, cols],
                start=True,
                stop=True,
            )

        def sum_squares(i, halves):
            squared = new(f"squared{i}_{halves[-1]}", [P, len(halves) * HALF], BF16)
            nc.scalar.activation(
                out=squared[:],
                in_=sums[i][:, halves[0] * HALF : (halves[-1] + 1) * HALF],
                func=ACT.Square,
                accum_out=squares[:, halves[-1], i : i + 1],
            )

        q_bf = round_queries()
        cs = gather_packed(cs_pool, U8, "cs")
        q_words = new("q_words", [P, QUERIES], U32)
        q_scales = new("q_scales", [P, QUERIES], U8)
        quantise(q_words[:], q_scales[:], q_bf[:].rearrange("p i m j -> p (i m j)"))
        cw = gather_packed(cw_pool, U32, "cw")
        ks = gather_packed(ks_pool, U8, "ks")
        kw = gather_packed(kw_pool, U32, "kw")
        for i in range(TILES):
            second[i] = exp_scores(i, scores(i, bank(i, [P, SLOTS]), cw, cs[:]), neg_l2, f"second{i}")
        for i in range(TILES):
            first[i] = exp_scores(i, scores(i, bank(TILES + i, [P, SLOTS]), kw, ks[K_ROW0:P, :]), neg_ls, f"first{i}")
        load_rsqrt_table()
        for i in range(TILES):
            take(i)
        v_pair = new("v_pair", [P, 2, P, PACK], BF16)
        turn_weights(0)
        gather_values(0)
        copy_values(0)
        round_weights(0)
        turn_weights(1)
        gather_values(1)
        copy_values(1)
        turn_weights(2)
        turn_weights(3)
        quantise_weights(0)
        round_weights(1)
        round_weights(2)
        quantise_weights(1)
        quantise_values([0, 1], v_pair[:].rearrange("p k e t -> p (k e t)"))
        round_weights(3)
        quantise_weights(2)
        gather_values(2)
        for i in range(TILES - 1):
            product(i, 0)
        gather_values(3)
        quantise_weights(3)
        copy_values(2)
        sum_squares(0, [0])
        sum_squares(1, [0])
        copy_values(3)
        sum_squares(2, [0])
        nc.scalar.activation(out=early[:], in_=squares[:, 0, :SPLIT_TILES], func=ACT.Identity, scale=1.0 / DV, bias=eps[:])
        quantise_values([2], v_bf[2][:].rearrange("p e t -> p (e t)"))
        product(0, 1, slice(0, P))
        quantise_values([3], v_bf[3][:].rearrange("p e t -> p (e t)"))

        rows_out = out[0].rearrange("(m i) e -> m i e", i=TILES)
        for i in range(TILES):
            split = i < SPLIT_TILES
            halves = [1] if split else [0, 1]
            for h in halves:
                product(i, h, slice(P if i == 0 else 0, HALF))
            sum_squares(i, halves)
            rstd = new(f"rstd{i}", [P, 1], F32)
            nc.scalar.activation(
                out=rstd[:],
                in_=squares[:, 1, i : i + 1],
                func=ACT.Abs_reciprocal_sqrt,
                scale=1.0 / DV,
                bias=early[:, i : i + 1] if split else eps[:],
            )
            result = new(f"result{i}", [P, DV], F32)
            if i < TILES - 1:
                nc.vector.tensor_scalar(out=result[:], in0=sums[i][:], scalar1=rstd[:], scalar2=None, op0=ALU.mult)
            else:
                nc.scalar.activation(out=result[:], in_=sums[i][:], func=ACT.Copy, scale=rstd[:])
            nc.sync.dma_start(out=rows_out[:, i, :], in_=result[:])
